import numpy as np
import ml_dtypes


def mxq(x, axis, fmt="e4m3"):
    dtype, down = {"e4m3": (ml_dtypes.float8_e4m3fn, 7), "e5m2": (ml_dtypes.float8_e5m2, 14)}[fmt]
    v = np.moveaxis(np.asarray(x, np.float32).astype(ml_dtypes.bfloat16).astype(np.float64), axis, -1)
    blocks = v.reshape(v.shape[:-1] + (-1, 32))
    amax = np.abs(blocks).max(-1, keepdims=True)
    byte = np.maximum(np.where(amax > 0, np.frexp(amax)[1] - 1 + 127, 0) - down, 1)
    scale = np.exp2(byte - 127.0)
    codes = (blocks / scale).astype(np.float32).astype(dtype).astype(np.float64)
    return np.moveaxis((codes * scale).reshape(v.shape), -1, axis)


WIDE = False


def mx_kscale(k):
    if not WIDE:
        return np.ones(k)
    levels = np.array([10, -10, 5, -5, 0])
    if k % 512:
        return np.exp2(np.random.permutation(np.resize(levels, k // 32))).repeat(32)
    a = np.empty((k // 512, 16))
    for p in range(k // 512):
        a[p, :8] = np.random.permutation(np.resize(levels, 8))
        for g in range(8):
            far = levels[np.abs(levels - a[p, g]) >= 10]
            a[p, g + 8] = far[np.random.randint(len(far))]
    return np.exp2(a.ravel()).repeat(32)


def f64(x):
    return np.asarray(x).astype(np.float64)


def striped(idx):
    return np.tile(idx.reshape(-1, 16).T, (8, 1)).astype(np.uint16)


def unstriped(offs):
    return offs[:16].T.reshape(-1).astype(np.int64)


E2M1 = np.array([0.0, 0.5, 1.0, 1.5, 2.0, 3.0, 4.0, 6.0, -0.0, -0.5, -1.0, -1.5, -2.0, -3.0, -4.0, -6.0])


def pack_weight(w, fmt):
    k, n = w.shape
    w = f64(np.asarray(w, np.float32).astype(ml_dtypes.bfloat16)).reshape(k // 32, 32, n)
    amax = np.abs(w).max(1)
    if fmt == "e4m3":
        byte = np.frexp(amax)[1] - 1 + 127 - 7
    else:
        mant, ex = np.frexp(amax / 6.0)
        byte = np.where(mant > 0.5, ex, ex - 1) + 127
    byte = np.clip(np.where(amax > 0, byte, 1), 1, 254)
    scaled = (w * np.exp2(127.0 - byte)[:, None, :]).reshape(k, n).astype(np.float32)
    by_word = np.ascontiguousarray(scaled.reshape(k // 512, 128, 4, n).transpose(0, 1, 3, 2))
    if fmt == "e4m3":
        words = by_word.astype(ml_dtypes.float8_e4m3fn).view(np.uint8)
    else:
        c = by_word.astype(ml_dtypes.float4_e2m1fn).view(np.uint8) & 0xF
        words = (c[..., 0::2] | (c[..., 1::2] << 4)).reshape(k // 512, 128, 2 * n)
    return np.ascontiguousarray(words), np.ascontiguousarray(byte.astype(np.uint8).reshape(k // 512, 16, n))


def unpack_weight(words, scales, fmt):
    g, _, n = scales.shape
    words = np.ascontiguousarray(words).reshape(g, 128, n, -1)
    if fmt == "e4m3":
        vals = words.view(ml_dtypes.float8_e4m3fn).astype(np.float64)
    else:
        nib = np.empty((g, 128, n, 4), np.uint8)
        nib[..., 0::2] = words & 0xF
        nib[..., 1::2] = words >> 4
        vals = E2M1[nib]
    vals = vals * np.repeat(np.exp2(scales.astype(np.float64) - 127.0), 8, axis=1)[..., None]
    return vals.transpose(0, 1, 3, 2).reshape(g * 512, n)


def split(x):
    m, e = np.frexp(f64(x))
    hi = np.ldexp(np.trunc(16.0 * m) / 16.0, e)
    return hi, f64(x) - hi


def gelu(v):
    return 0.5 * v * (1.0 + np.tanh(np.sqrt(2.0 / np.pi) * (v + 0.044715 * v**3)))


K, M, T, S = 1024, 1024, 2048, 1024


def setup_inputs():
    n = np.random.standard_normal
    s = mx_kscale(K)[:, None]
    v = pack_weight(n((K, T)) * s, "e4m3")
    return {
        "tab_words": v[0],
        "tab_scales": v[1],
        "w": (n((K, M)) / np.sqrt(K) / s).astype(np.float32),
        "ts": np.tile(np.exp(0.5 * n(T)), (128, 1)).astype(np.float32),
        "b": (0.3 * n(1024)).astype(np.float32),
        "offs": striped(np.random.permutation(T)[:S]),
    }


def reference(tab_words, tab_scales, w, ts, b, offs):
    tab_ = unpack_weight(tab_words, tab_scales, "e4m3")[:, unstriped(offs)]
    w_hi, w_lo = split(w)
    w_hi_, w_lo_ = mxq(w_hi, 0, "e4m3"), mxq(w_lo, 0, "e4m3")
    y = w_hi_.T @ tab_ + w_lo_.T @ tab_
    y = y * f64(ts)[0][unstriped(offs)]
    return gelu(y + f64(b)[:, None])

@@ -1,0 +1,158 @@
+from contextlib import ExitStack
+
+import concourse.mybir as mybir
+
+K, M, T, S = 1024, 1024, 2048, 1024
+FLOPS = 2 * 2 * K * M * S
+
+F32 = mybir.dt.float32
+BF16 = mybir.dt.bfloat16
+I32 = mybir.dt.int32
+U32 = mybir.dt.uint32
+U16 = mybir.dt.uint16
+U8 = mybir.dt.uint8
+FP8X4 = mybir.dt.float8_e4m3fn_x4
+ALU = mybir.AluOpType
+ACT = mybir.ActivationFunctionType
+
+P = 128
+PACK = 4
+PASSES = K // (P * PACK)
+NQ = 256
+QUARTERS = M // NQ
+JH = 512
+HALVES = S // JH
+HI_MASK = 0xFFF0FFF0 - (1 << 32)
+POOL_SUBS = ((0, 0), (1, 0), (0, 1), (1, 1), (0, 2), (1, 2), (0, 3))
+
+
+def tile_list_tabts_gelu_kernel(tc, tab_words, tab_scales, w, ts, b, offs, out):
+    nc = tc.nc
+    with ExitStack() as ctx:
+        keep = ctx.enter_context(tc.tile_pool(name="keep", bufs=1))
+        work = ctx.enter_context(tc.tile_pool(name="work", bufs=8))
+        psum = ctx.enter_context(tc.psum_pool(name="psum", bufs=8))
+
+        chunks = [(a, q) for q in range(QUARTERS) for a in range(PASSES)]
+        offsets = keep.tile([P, S // 16], U16, name="offsets")
+        words = [keep.tile([P, T], I32, name="words%d" % a, align_bytes=64) for a in range(PASSES)]
+        plane = keep.tile([P, T // 4], I32, name="plane", align_bytes=64)
+        ts_all = keep.tile([P, T], F32, name="ts_all", align_bytes=64)
+        bias = keep.tile([P, M // P], F32, name="bias")
+        warm = keep.tile([P, 8], F32, name="warm")
+        w_raw = {c: keep.tile([P, PACK, NQ], F32, name="w_raw%d%d" % c, align_bytes=64) for c in chunks}
+        parts = {c: keep.tile([P, 2, NQ, PACK], BF16, name="parts%d%d" % c, align_bytes=64) for c in chunks}
+        w_codes = {c: keep.tile([P, 2 * NQ], U32, name="w_codes%d%d" % c, align_bytes=64) for c in chunks}
+        w_scales = {c: keep.tile([P, 2 * NQ], U8, name="w_scales%d%d" % c, align_bytes=64) for c in chunks}
+        v_codes = {(a, h): keep.tile([P, JH], U32, name="v_codes%d%d" % (a, h), align_bytes=64)
+                   for a in range(PASSES) for h in range(HALVES)}
+        v_scales = [keep.tile([P, JH], U8, name="v_scales%d" % h, align_bytes=64) for h in range(HALVES)]
+        ts_picked = [keep.tile([P, JH], F32, name="ts_picked%d" % h, align_bytes=64) for h in range(HALVES)]
+        acc = {}
+
+        def load_w(c):
+            a, q = c
+            rows = w[a * P * PACK:(a + 1) * P * PACK, q * NQ:(q + 1) * NQ]
+            nc.sync.dma_start(out=w_raw[c][:], in_=rows.rearrange("(p t) n -> p t n", t=PACK))
+
+        def load_words(a):
+            nc.sync.dma_start(out=words[a][:], in_=tab_words[a].rearrange("p t i -> p (t i)").bitcast(I32))
+
+        def load_scales():
+            for quad in range(4):
+                nc.sync.dma_start(out=plane[32 * quad:32 * quad + 4 * PASSES, :],
+                                  in_=tab_scales[:, 4 * quad:4 * quad + 4, :].bitcast(I32))
+
+        def picks(h):
+            return offsets[:, h * JH // 16:(h + 1) * JH // 16]
+
+        def gather_words(a, h):
+            nc.vector.tensor_copy(v_codes[a, h][:], words[a][:].bitcast(U32).indirect(picks(h)))
+
+        def gather_scales(h):
+            nc.vector.tensor_copy(v_scales[h][:], plane[:].bitcast(U8).indirect(picks(h)))
+
+        def gather_ts(h):
+            nc.vector.tensor_copy(ts_picked[h][:], ts_all[:].indirect(picks(h)))
+
+        def truncate(c):
+            upper = w_raw[c][:].bitcast(BF16).rearrange("p t (n i e) -> p n t i e", i=4, e=2)[:, :, :, :, 1]
+            nc.scalar.copy(out=parts[c][:, 0].rearrange("p (n i) t -> p n t i", i=4), in_=upper)
+
+        def mask(c):
+            pairs = parts[c][:, 0].rearrange("p n t -> p (n t)").bitcast(I32)
+            nc.vector.tensor_scalar(pairs, pairs, HI_MASK, None, ALU.bitwise_and)
+
+        def subtract(c):
+            engine = nc.gpsimd if c in POOL_SUBS else nc.vector
+            engine.tensor_tensor(parts[c][:, 1], w_raw[c][:].rearrange("p t n -> p n t"), parts[c][:, 0], ALU.subtract)
+
+        def quantize(c):
+            nc.vector.quantize_mx(out=w_codes[c][:].bitcast(FP8X4), scales=w_scales[c][:],
+                                  in_=parts[c][:].rearrange("p s n t -> p (s n t)"))
+
+        def multiply(c):
+            a, q = c
+            for i in range(NQ // P):
+                for h in range(HALVES):
+                    if a == 0:
+                        acc[q, i, h] = psum.tile([P, JH], F32, name="acc")
+                    for s in range(2):
+                        cols = slice(s * NQ + i * P, s * NQ + (i + 1) * P)
+                        nc.tensor.matmul_mx(out=acc[q, i, h][:], lhsT=w_codes[c][:, cols].bitcast(FP8X4),
+                                            lhsT_scale=w_scales[c][:, cols], rhs=v_codes[a, h][:].bitcast(FP8X4),
+                                            rhs_scale=v_scales[h][4 * a:, :],
+                                            start=(a == 0 and s == 0), stop=(a == PASSES - 1 and s == 1))
+
+        def finish(q):
+            for i in range(NQ // P):
+                n = q * (NQ // P) + i
+                for h in range(HALVES):
+                    scaled = work.tile([P, JH], F32, name="scaled")
+                    nc.vector.tensor_tensor(scaled[:], acc[q, i, h][:], ts_picked[h][:], ALU.mult)
+                    result = work.tile([P, JH], F32, name="result")
+                    nc.scalar.activation(result[:], scaled[:], ACT.Gelu_apprx_tanh, bias=bias[:, n:n + 1])
+                    nc.sync.dma_start(out=out[n * P:(n + 1) * P, h * JH:(h + 1) * JH], in_=result[:])
+
+        nc.vector.memset(plane[:], 0)
+        nc.gpsimd.memset(warm[:], 0.0)
+        nc.scalar.activation(warm[:, 4:5], warm[:, 0:1], ACT.Gelu_apprx_tanh)
+        nc.sync.dma_start(offsets[:], offs)
+        load_w(chunks[0])
+        load_words(0)
+        load_scales()
+        load_w(chunks[1])
+        load_words(1)
+        load_w(chunks[2])
+        nc.sync.dma_start(out=ts_all[:], in_=ts)
+        load_w(chunks[3])
+        with nc.allow_non_contiguous_dma(reason="one bias value for each partition"):
+            nc.sync.dma_start(out=bias[:], in_=b.rearrange("(c p) -> p c", p=P))
+        for c in chunks[4:]:
+            load_w(c)
+        for c in chunks:
+            truncate(c)
+
+        def step(c, beside):
+            mask(c)
+            subtract(c)
+            beside()
+            quantize(c)
+
+        step(chunks[0], lambda: [gather_words(0, h) for h in range(HALVES)])
+        step(chunks[1], lambda: [gather_scales(h) for h in range(HALVES)])
+        multiply(chunks[0])
+        step(chunks[2], lambda: [gather_words(1, h) for h in range(HALVES)])
+        multiply(chunks[1])
+        multiply(chunks[2])
+        step(chunks[3], lambda: [gather_ts(h) for h in range(HALVES)])
+        multiply(chunks[3])
+        step(chunks[4], lambda: finish(0))
+        multiply(chunks[4])
+        step(chunks[5], lambda: finish(1))
+        multiply(chunks[5])
+        step(chunks[6], lambda: finish(2))
+        multiply(chunks[6])
+        step(chunks[7], lambda: None)
+        multiply(chunks[7])
+        finish(3)

@@ -1,6 +1,7 @@
 from contextlib import ExitStack
 
 import concourse.mybir as mybir
+from concourse.masks import make_identity
 
 K, M, T, S = 1024, 1024, 2048, 1024
 FLOPS = 2 * 2 * K * M * S
@@ -22,24 +23,29 @@ NQ = 256
 QUARTERS = M // NQ
 JH = 512
 HALVES = S // JH
+RUN = 4
 HI_MASK = 0xFFF0FFF0 - (1 << 32)
-POOL_SUBS = ((0, 0), (1, 0), (0, 1), (1, 1), (0, 2), (1, 2), (0, 3))
+VECTOR_COLUMNS = NQ // 4
+STAGING_BUFS = 8
+PSUM_BANKS = 8
 
 
 def tile_list_tabts_gelu_kernel(tc, tab_words, tab_scales, w, ts, b, offs, out):
     nc = tc.nc
     with ExitStack() as ctx:
         keep = ctx.enter_context(tc.tile_pool(name="keep", bufs=1))
-        work = ctx.enter_context(tc.tile_pool(name="work", bufs=8))
-        psum = ctx.enter_context(tc.psum_pool(name="psum", bufs=8))
+        work = ctx.enter_context(tc.tile_pool(name="work", bufs=STAGING_BUFS))
+        psum = ctx.enter_context(tc.psum_pool(name="psum", bufs=PSUM_BANKS))
 
         chunks = [(a, q) for q in range(QUARTERS) for a in range(PASSES)]
         offsets = keep.tile([P, S // 16], U16, name="offsets")
-        words = [keep.tile([P, T], I32, name="words%d" % a, align_bytes=64) for a in range(PASSES)]
-        plane = keep.tile([P, T // 4], I32, name="plane", align_bytes=64)
+        table_words = [keep.tile([P, T], I32, name="table_words%d" % a, align_bytes=64) for a in range(PASSES)]
+        table_scales = keep.tile([P, T // 4], I32, name="table_scales", align_bytes=64)
         ts_all = keep.tile([P, T], F32, name="ts_all", align_bytes=64)
+        bias_rows = keep.tile([P, P], F32, name="bias_rows")
         bias = keep.tile([P, M // P], F32, name="bias")
         warm = keep.tile([P, 8], F32, name="warm")
+        identity = keep.tile([P, P], F32, name="identity")
         w_raw = {c: keep.tile([P, PACK, NQ], F32, name="w_raw%d%d" % c, align_bytes=64) for c in chunks}
         parts = {c: keep.tile([P, 2, NQ, PACK], BF16, name="parts%d%d" % c, align_bytes=64) for c in chunks}
         w_codes = {c: keep.tile([P, 2 * NQ], U32, name="w_codes%d%d" % c, align_bytes=64) for c in chunks}
@@ -48,111 +54,206 @@ def tile_list_tabts_gelu_kernel(tc, tab_words, tab_scales, w, ts, b, offs, out):
                    for a in range(PASSES) for h in range(HALVES)}
         v_scales = [keep.tile([P, JH], U8, name="v_scales%d" % h, align_bytes=64) for h in range(HALVES)]
         ts_picked = [keep.tile([P, JH], F32, name="ts_picked%d" % h, align_bytes=64) for h in range(HALVES)]
-        acc = {}
+        ts_turned = keep.tile([P, JH // P], F32, name="ts_turned")
+        sums = {}
+        turned = {}
 
-        def load_w(c):
-            a, q = c
+        def load_w(a, q):
             rows = w[a * P * PACK:(a + 1) * P * PACK, q * NQ:(q + 1) * NQ]
-            nc.sync.dma_start(out=w_raw[c][:], in_=rows.rearrange("(p t) n -> p t n", t=PACK))
+            nc.sync.dma_start(out=w_raw[a, q][:], in_=rows.rearrange("(p t) n -> p t n", t=PACK))
 
         def load_words(a):
-            nc.sync.dma_start(out=words[a][:], in_=tab_words[a].rearrange("p t i -> p (t i)").bitcast(I32))
+            nc.sync.dma_start(out=table_words[a][:], in_=tab_words[a].rearrange("p t i -> p (t i)").bitcast(I32))
 
         def load_scales():
             for quad in range(4):
-                nc.sync.dma_start(out=plane[32 * quad:32 * quad + 4 * PASSES, :],
+                nc.sync.dma_start(out=table_scales[32 * quad:32 * quad + 4 * PASSES, :],
                                   in_=tab_scales[:, 4 * quad:4 * quad + 4, :].bitcast(I32))
+
+        def load_bias():
+            rows = b.rearrange("(r p) -> r p", p=P).unsqueeze(0).to_broadcast([P * P // M, M // P, P])
+            nc.sync.dma_start(out=bias_rows[:], in_=rows)
+            bank = psum.tile([P, P], F32, name="bank")
+            nc.tensor.transpose(bank[:], bias_rows[:], identity[:])
+            nc.scalar.copy(out=bias[:], in_=bank[:, :M // P])
 
         def picks(h):
             return offsets[:, h * JH // 16:(h + 1) * JH // 16]
 
         def gather_words(a, h):
-            nc.vector.tensor_copy(v_codes[a, h][:], words[a][:].bitcast(U32).indirect(picks(h)))
+            nc.vector.tensor_copy(v_codes[a, h][:], table_words[a][:].bitcast(U32).indirect(picks(h)))
 
         def gather_scales(h):
-            nc.vector.tensor_copy(v_scales[h][:], plane[:].bitcast(U8).indirect(picks(h)))
+            nc.vector.tensor_copy(v_scales[h][:], table_scales[:].bitcast(U8).indirect(picks(h)))
 
         def gather_ts(h):
             nc.vector.tensor_copy(ts_picked[h][:], ts_all[:].indirect(picks(h)))
 
-        def truncate(c):
-            upper = w_raw[c][:].bitcast(BF16).rearrange("p t (n i e) -> p n t i e", i=4, e=2)[:, :, :, :, 1]
-            nc.scalar.copy(out=parts[c][:, 0].rearrange("p (n i) t -> p n t i", i=4), in_=upper)
+        def truncate(a, q, copy=nc.scalar.copy):
+            upper = w_raw[a, q][:].bitcast(BF16).rearrange("p t (n i e) -> p n t i e", i=RUN, e=2)[:, :, :, :, 1]
+            copy(out=parts[a, q][:, 0].rearrange("p (n i) t -> p n t i", i=RUN), in_=upper)
 
-        def mask(c):
-            pairs = parts[c][:, 0].rearrange("p n t -> p (n t)").bitcast(I32)
+        def mask(a, q, cols=slice(0, NQ)):
+            pairs = parts[a, q][:, 0, cols].rearrange("p n t -> p (n t)").bitcast(I32)
             nc.vector.tensor_scalar(pairs, pairs, HI_MASK, None, ALU.bitwise_and)
 
-        def subtract(c):
-            engine = nc.gpsimd if c in POOL_SUBS else nc.vector
-            engine.tensor_tensor(parts[c][:, 1], w_raw[c][:].rearrange("p t n -> p n t"), parts[c][:, 0], ALU.subtract)
+        def subtract(a, q, cols=slice(0, NQ)):
+            nc.vector.tensor_tensor(parts[a, q][:, 1, cols].rearrange("p (n i) t -> p n t i", i=RUN),
+                                    w_raw[a, q][:, :, cols].rearrange("p t (n i) -> p n t i", i=RUN),
+                                    parts[a, q][:, 0, cols].rearrange("p (n i) t -> p n t i", i=RUN), ALU.subtract)
 
-        def quantize(c):
-            nc.vector.quantize_mx(out=w_codes[c][:].bitcast(FP8X4), scales=w_scales[c][:],
-                                  in_=parts[c][:].rearrange("p s n t -> p (s n t)"))
+        def split_with_gpsimd(a, q):
+            own, rest = slice(0, VECTOR_COLUMNS), slice(VECTOR_COLUMNS, NQ)
+            mask(a, q, own)
+            mask(a, q, rest)
+            subtract(a, q, own)
+            nc.gpsimd.tensor_tensor(parts[a, q][:, 1, rest], w_raw[a, q][:, :, rest].rearrange("p t n -> p n t"),
+                                    parts[a, q][:, 0, rest], ALU.subtract)
 
-        def multiply(c):
-            a, q = c
+        def quantize(a, q):
+            nc.vector.quantize_mx(out=w_codes[a, q][:].bitcast(FP8X4), scales=w_scales[a, q][:],
+                                  in_=parts[a, q][:].rearrange("p s n t -> p (s n t)"))
+
+        def multiply(a, q, h):
             for i in range(NQ // P):
-                for h in range(HALVES):
-                    if a == 0:
-                        acc[q, i, h] = psum.tile([P, JH], F32, name="acc")
+                if a == 0:
+                    sums[q, h, i] = psum.tile([P, JH], F32, name="bank")
+                for s in range(2):
+                    cols = slice(s * NQ + i * P, s * NQ + (i + 1) * P)
+                    nc.tensor.matmul_mx(out=sums[q, h, i][:], lhsT=w_codes[a, q][:, cols].bitcast(FP8X4),
+                                        lhsT_scale=w_scales[a, q][:, cols], rhs=v_codes[a, h][:].bitcast(FP8X4),
+                                        rhs_scale=v_scales[h][4 * a:, :],
+                                        start=(a == 0 and s == 0), stop=(a == PASSES - 1 and s == 1))
+
+        def activate(source, q, i, cols, queue=nc.sync):
+            r = q * (NQ // P) + i
+            result = work.tile([P, cols.stop - cols.start], F32, name="result")
+            nc.scalar.activation(result[:], source, ACT.Gelu_apprx_tanh, bias=bias[:, r:r + 1])
+            queue.dma_start(out=out[r * P:(r + 1) * P, cols], in_=result[:])
+
+        def finish(q, h, i, cols=slice(0, JH), queue=nc.sync):
+            scaled = work.tile([P, cols.stop - cols.start], F32, name="scaled")
+            nc.vector.tensor_tensor(scaled[:], sums[q, h, i][:, cols], ts_picked[h][:, cols], ALU.mult)
+            activate(scaled[:], q, i, slice(h * JH + cols.start, h * JH + cols.stop), queue)
+
+        def turn_ts():
+            bank = psum.tile([P, JH // P, P], F32, name="bank")
+            for g in range(JH // P):
+                nc.tensor.transpose(bank[:, g, :], ts_picked[0][:, g * P:(g + 1) * P], identity[:])
+            nc.scalar.copy(out=ts_turned[:], in_=bank[:, :, 0])
+
+        def multiply_turned(q):
+            for g in range(JH // P):
+                if g % 2 == 0:
+                    sums[q, 0, g // 2] = psum.tile([P, 2, NQ], F32, name="bank")
+                entries = slice(g * P, (g + 1) * P)
+                for a in range(PASSES):
                     for s in range(2):
-                        cols = slice(s * NQ + i * P, s * NQ + (i + 1) * P)
-                        nc.tensor.matmul_mx(out=acc[q, i, h][:], lhsT=w_codes[c][:, cols].bitcast(FP8X4),
-                                            lhsT_scale=w_scales[c][:, cols], rhs=v_codes[a, h][:].bitcast(FP8X4),
-                                            rhs_scale=v_scales[h][4 * a:, :],
+                        cols = slice(s * NQ, (s + 1) * NQ)
+                        nc.tensor.matmul_mx(out=sums[q, 0, g // 2][:, g % 2, :],
+                                            lhsT=v_codes[a, 0][:, entries].bitcast(FP8X4),
+                                            lhsT_scale=v_scales[0][4 * a:, entries],
+                                            rhs=w_codes[a, q][:, cols].bitcast(FP8X4), rhs_scale=w_scales[a, q][:, cols],
                                             start=(a == 0 and s == 0), stop=(a == PASSES - 1 and s == 1))
 
-        def finish(q):
-            for i in range(NQ // P):
-                n = q * (NQ // P) + i
-                for h in range(HALVES):
-                    scaled = work.tile([P, JH], F32, name="scaled")
-                    nc.vector.tensor_tensor(scaled[:], acc[q, i, h][:], ts_picked[h][:], ALU.mult)
-                    result = work.tile([P, JH], F32, name="result")
-                    nc.scalar.activation(result[:], scaled[:], ACT.Gelu_apprx_tanh, bias=bias[:, n:n + 1])
-                    nc.sync.dma_start(out=out[n * P:(n + 1) * P, h * JH:(h + 1) * JH], in_=result[:])
+        def scale_turned(q):
+            turned[q] = keep.tile([P, JH // P, NQ], F32, name="turned%d" % q)
+            for g in range(JH // P):
+                nc.scalar.activation(turned[q][:, g, :], sums[q, 0, g // 2][:, g % 2, :], ACT.Copy,
+                                     scale=ts_turned[:, g:g + 1])
 
-        nc.vector.memset(plane[:], 0)
+        def finish_turned(q):
+            banks = [psum.tile([P, JH], F32, name="bank") for i in range(NQ // P)]
+            for i in range(NQ // P):
+                for g in range(JH // P):
+                    nc.tensor.transpose(banks[i][:, g * P:(g + 1) * P], turned[q][:, g, i * P:(i + 1) * P], identity[:])
+            for i in range(NQ // P):
+                activate(banks[i][:], q, i, slice(0, JH))
+
+        nc.gpsimd.memset(table_scales[:, :T // 8], 0)
+        nc.vector.memset(table_scales[:, T // 8:], 0)
         nc.gpsimd.memset(warm[:], 0.0)
         nc.scalar.activation(warm[:, 4:5], warm[:, 0:1], ACT.Gelu_apprx_tanh)
+        make_identity(nc, identity[:])
         nc.sync.dma_start(offsets[:], offs)
-        load_w(chunks[0])
-        load_words(0)
+        load_w(0, 0)
         load_scales()
-        load_w(chunks[1])
+        load_w(1, 0)
+        load_bias()
+        load_words(0)
+        load_w(0, 1)
         load_words(1)
-        load_w(chunks[2])
+        load_w(1, 1)
         nc.sync.dma_start(out=ts_all[:], in_=ts)
-        load_w(chunks[3])
-        with nc.allow_non_contiguous_dma(reason="one bias value for each partition"):
-            nc.sync.dma_start(out=bias[:], in_=b.rearrange("(c p) -> p c", p=P))
-        for c in chunks[4:]:
-            load_w(c)
-        for c in chunks:
-            truncate(c)
-
-        def step(c, beside):
-            mask(c)
-            subtract(c)
-            beside()
-            quantize(c)
-
-        step(chunks[0], lambda: [gather_words(0, h) for h in range(HALVES)])
-        step(chunks[1], lambda: [gather_scales(h) for h in range(HALVES)])
-        multiply(chunks[0])
-        step(chunks[2], lambda: [gather_words(1, h) for h in range(HALVES)])
-        multiply(chunks[1])
-        multiply(chunks[2])
-        step(chunks[3], lambda: [gather_ts(h) for h in range(HALVES)])
-        multiply(chunks[3])
-        step(chunks[4], lambda: finish(0))
-        multiply(chunks[4])
-        step(chunks[5], lambda: finish(1))
-        multiply(chunks[5])
-        step(chunks[6], lambda: finish(2))
-        multiply(chunks[6])
-        step(chunks[7], lambda: None)
-        multiply(chunks[7])
-        finish(3)
+        load_w(0, 2)
+        load_w(1, 2)
+        load_w(0, 3)
+        load_w(1, 3)
+        truncate(0, 0, nc.vector.tensor_copy)
+        truncate(1, 0)
+        truncate(0, 1)
+        truncate(1, 1)
+        truncate(0, 2)
+        truncate(1, 2)
+        split_with_gpsimd(0, 0)
+        gather_scales(1)
+        gather_scales(0)
+        quantize(0, 0)
+        split_with_gpsimd(1, 0)
+        gather_words(0, 1)
+        multiply(0, 0, 1)
+        gather_words(0, 0)
+        quantize(1, 0)
+        split_with_gpsimd(0, 1)
+        gather_words(1, 1)
+        multiply(1, 0, 1)
+        gather_words(1, 0)
+        multiply_turned(0)
+        quantize(0, 1)
+        multiply(0, 1, 1)
+        split_with_gpsimd(1, 1)
+        gather_ts(0)
+        turn_ts()
+        gather_ts(1)
+        quantize(1, 1)
+        multiply(1, 1, 1)
+        multiply_turned(1)
+        finish(0, 1, 0)
+        scale_turned(0)
+        mask(0, 2)
+        finish(0, 1, 1)
+        truncate(0, 3)
+        truncate(1, 3)
+        finish_turned(0)
+        subtract(0, 2)
+        mask(1, 2)
+        quantize(0, 2)
+        multiply(0, 2, 0)
+        multiply(0, 2, 1)
+        subtract(1, 2)
+        finish(1, 1, 0)
+        scale_turned(1)
+        quantize(1, 2)
+        multiply(1, 2, 0)
+        multiply(1, 2, 1)
+        finish_turned(1)
+        mask(0, 3)
+        finish(1, 1, 1)
+        mask(1, 3)
+        subtract(0, 3)
+        finish(2, 0, 0)
+        quantize(0, 3)
+        multiply(0, 3, 0)
+        multiply(0, 3, 1)
+        subtract(1, 3)
+        finish(2, 0, 1)
+        quantize(1, 3)
+        multiply(1, 3, 0)
+        multiply(1, 3, 1)
+        finish(2, 1, 0)
+        finish(2, 1, 1)
+        finish(3, 0, 0)
+        finish(3, 0, 1)
+        finish(3, 1, 0)
+        finish(3, 1, 1, slice(0, JH // 2))
+        finish(3, 1, 1, slice(JH // 2, JH), nc.scalar)

@@ -175,26 +175,23 @@ def tile_list_tabts_gelu_kernel(tc, tab_words, tab_scales, w, ts, b, offs, out):
         nc.gpsimd.memset(warm[:], 0.0)
         nc.scalar.activation(warm[:, 4:5], warm[:, 0:1], ACT.Gelu_apprx_tanh)
         make_identity(nc, identity[:])
+
         nc.sync.dma_start(offsets[:], offs)
         load_w(0, 0)
         load_scales()
-        load_w(1, 0)
         load_bias()
+        load_w(1, 0)
         load_words(0)
         load_w(0, 1)
         load_words(1)
         load_w(1, 1)
         nc.sync.dma_start(out=ts_all[:], in_=ts)
-        load_w(0, 2)
-        load_w(1, 2)
-        load_w(0, 3)
-        load_w(1, 3)
+        for a, q in chunks[4:]:
+            load_w(a, q)
         truncate(0, 0, nc.vector.tensor_copy)
-        truncate(1, 0)
-        truncate(0, 1)
-        truncate(1, 1)
-        truncate(0, 2)
-        truncate(1, 2)
+        for a, q in chunks[1:6]:
+            truncate(a, q)
+
         split_with_gpsimd(0, 0)
         gather_scales(1)
         gather_scales(0)
@@ -205,51 +202,52 @@ def tile_list_tabts_gelu_kernel(tc, tab_words, tab_scales, w, ts, b, offs, out):
         gather_words(0, 0)
         quantize(1, 0)
         split_with_gpsimd(0, 1)
-        gather_words(1, 1)
-        multiply(1, 0, 1)
         gather_words(1, 0)
         multiply_turned(0)
+        gather_words(1, 1)
+        multiply(1, 0, 1)
         quantize(0, 1)
         multiply(0, 1, 1)
         split_with_gpsimd(1, 1)
         gather_ts(0)
         turn_ts()
-        gather_ts(1)
-        quantize(1, 1)
-        multiply(1, 1, 1)
-        multiply_turned(1)
-        finish(0, 1, 0)
         scale_turned(0)
-        mask(0, 2)
-        finish(0, 1, 1)
+        gather_ts(1)
         truncate(0, 3)
-        truncate(1, 3)
+        quantize(1, 1)
+        multiply_turned(1)
+        multiply(1, 1, 1)
+
+        mask(0, 2)
+        finish(0, 1, 0)
         finish_turned(0)
+        scale_turned(1)
+        truncate(1, 3)
         subtract(0, 2)
         mask(1, 2)
         quantize(0, 2)
-        multiply(0, 2, 0)
-        multiply(0, 2, 1)
-        subtract(1, 2)
-        finish(1, 1, 0)
-        scale_turned(1)
-        quantize(1, 2)
-        multiply(1, 2, 0)
-        multiply(1, 2, 1)
+        for h in range(HALVES):
+            multiply(0, 2, h)
         finish_turned(1)
+        subtract(1, 2)
+        finish(0, 1, 1)
+        finish(1, 1, 0)
+        quantize(1, 2)
+        for h in range(HALVES):
+            multiply(1, 2, h)
         mask(0, 3)
-        finish(1, 1, 1)
         mask(1, 3)
+        finish(1, 1, 1)
         subtract(0, 3)
         finish(2, 0, 0)
         quantize(0, 3)
-        multiply(0, 3, 0)
-        multiply(0, 3, 1)
+        for h in range(HALVES):
+            multiply(0, 3, h)
         subtract(1, 3)
         finish(2, 0, 1)
         quantize(1, 3)
-        multiply(1, 3, 0)
-        multiply(1, 3, 1)
+        for h in range(HALVES):
+            multiply(1, 3, h)
         finish(2, 1, 0)
         finish(2, 1, 1)
         finish(3, 0, 0)

@@ -25,7 +25,7 @@ JH = 512
 HALVES = S // JH
 RUN = 4
 HI_MASK = 0xFFF0FFF0 - (1 << 32)
-VECTOR_COLUMNS = NQ // 4
+VECTOR_COLUMNS = NQ // 8
 STAGING_BUFS = 8
 PSUM_BANKS = 8
 
@@ -48,6 +48,8 @@ def tile_list_tabts_gelu_kernel(tc, tab_words, tab_scales, w, ts, b, offs, out):
         identity = keep.tile([P, P], F32, name="identity")
         w_raw = {c: keep.tile([P, PACK, NQ], F32, name="w_raw%d%d" % c, align_bytes=64) for c in chunks}
         parts = {c: keep.tile([P, 2, NQ, PACK], BF16, name="parts%d%d" % c, align_bytes=64) for c in chunks}
+        w_woven = {c: keep.tile([P, NQ - VECTOR_COLUMNS, PACK], F32, name="w_woven%d%d" % c, align_bytes=64)
+                   for c in chunks[:4]}
         w_codes = {c: keep.tile([P, 2 * NQ], U32, name="w_codes%d%d" % c, align_bytes=64) for c in chunks}
         w_scales = {c: keep.tile([P, 2 * NQ], U8, name="w_scales%d%d" % c, align_bytes=64) for c in chunks}
         v_codes = {(a, h): keep.tile([P, JH], U32, name="v_codes%d%d" % (a, h), align_bytes=64)
@@ -93,6 +95,10 @@ def tile_list_tabts_gelu_kernel(tc, tab_words, tab_scales, w, ts, b, offs, out):
             upper = w_raw[a, q][:].bitcast(BF16).rearrange("p t (n i e) -> p n t i e", i=RUN, e=2)[:, :, :, :, 1]
             copy(out=parts[a, q][:, 0].rearrange("p (n i) t -> p n t i", i=RUN), in_=upper)
 
+        def weave(a, q):
+            nc.scalar.copy(out=w_woven[a, q][:].rearrange("p (n i) t -> p n t i", i=RUN),
+                           in_=w_raw[a, q][:, :, VECTOR_COLUMNS:].rearrange("p t (n i) -> p n t i", i=RUN))
+
         def mask(a, q, cols=slice(0, NQ)):
             pairs = parts[a, q][:, 0, cols].rearrange("p n t -> p (n t)").bitcast(I32)
             nc.vector.tensor_scalar(pairs, pairs, HI_MASK, None, ALU.bitwise_and)
@@ -107,8 +113,7 @@ def tile_list_tabts_gelu_kernel(tc, tab_words, tab_scales, w, ts, b, offs, out):
             mask(a, q, own)
             mask(a, q, rest)
             subtract(a, q, own)
-            nc.gpsimd.tensor_tensor(parts[a, q][:, 1, rest], w_raw[a, q][:, :, rest].rearrange("p t n -> p n t"),
-                                    parts[a, q][:, 0, rest], ALU.subtract)
+            nc.gpsimd.tensor_tensor(parts[a, q][:, 1, rest], w_woven[a, q][:], parts[a, q][:, 0, rest], ALU.subtract)
 
         def quantize(a, q):
             nc.vector.quantize_mx(out=w_codes[a, q][:].bitcast(FP8X4), scales=w_scales[a, q][:],
@@ -189,7 +194,11 @@ def tile_list_tabts_gelu_kernel(tc, tab_words, tab_scales, w, ts, b, offs, out):
         for a, q in chunks[4:]:
             load_w(a, q)
         truncate(0, 0, nc.vector.tensor_copy)
-        for a, q in chunks[1:6]:
+        weave(0, 0)
+        for a, q in chunks[1:4]:
+            truncate(a, q)
+            weave(a, q)
+        for a, q in chunks[4:6]:
             truncate(a, q)
 
         split_with_gpsimd(0, 0)

@@ -27,7 +27,7 @@ RUN = 4
 HI_MASK = 0xFFF0FFF0 - (1 << 32)
 VECTOR_COLUMNS = NQ // 8
 STAGING_BUFS = 8
-PSUM_BANKS = 8
+BANK_BYTES = 4 * JH
 
 
 def tile_list_tabts_gelu_kernel(tc, tab_words, tab_scales, w, ts, b, offs, out):
@@ -35,7 +35,8 @@ def tile_list_tabts_gelu_kernel(tc, tab_words, tab_scales, w, ts, b, offs, out):
     with ExitStack() as ctx:
         keep = ctx.enter_context(tc.tile_pool(name="keep", bufs=1))
         work = ctx.enter_context(tc.tile_pool(name="work", bufs=STAGING_BUFS))
-        psum = ctx.enter_context(tc.psum_pool(name="psum", bufs=PSUM_BANKS))
+        psum = ctx.enter_context(tc.psum_pool(name="psum", bufs=1))
+        shared = ctx.enter_context(tc.tile_pool(name="shared", bufs=1))
 
         chunks = [(a, q) for q in range(QUARTERS) for a in range(PASSES)]
         offsets = keep.tile([P, S // 16], U16, name="offsets")
@@ -49,7 +50,7 @@ def tile_list_tabts_gelu_kernel(tc, tab_words, tab_scales, w, ts, b, offs, out):
         w_raw = {c: keep.tile([P, PACK, NQ], F32, name="w_raw%d%d" % c, align_bytes=64) for c in chunks}
         parts = {c: keep.tile([P, 2, NQ, PACK], BF16, name="parts%d%d" % c, align_bytes=64) for c in chunks}
         w_woven = {c: keep.tile([P, NQ - VECTOR_COLUMNS, PACK], F32, name="w_woven%d%d" % c, align_bytes=64)
-                   for c in chunks[:4]}
+                   for c in chunks[:5] + chunks[7:]}
         w_codes = {c: keep.tile([P, 2 * NQ], U32, name="w_codes%d%d" % c, align_bytes=64) for c in chunks}
         w_scales = {c: keep.tile([P, 2 * NQ], U8, name="w_scales%d%d" % c, align_bytes=64) for c in chunks}
         v_codes = {(a, h): keep.tile([P, JH], U32, name="v_codes%d%d" % (a, h), align_bytes=64)
@@ -57,6 +58,26 @@ def tile_list_tabts_gelu_kernel(tc, tab_words, tab_scales, w, ts, b, offs, out):
         v_scales = [keep.tile([P, JH], U8, name="v_scales%d" % h, align_bytes=64) for h in range(HALVES)]
         ts_picked = [keep.tile([P, JH], F32, name="ts_picked%d" % h, align_bytes=64) for h in range(HALVES)]
         ts_turned = keep.tile([P, JH // P], F32, name="ts_turned")
+        upper, staged = {}, {}
+        for n, (c, tiles) in enumerate((((0, 2), ((0, 1), (1, 1))), ((1, 3), ((1, 0), (2, 0))))):
+            upper[c] = shared.tile([P, 4, NQ, PACK], BF16, name="upper%d" % n, align_bytes=64, offset=n * 4 * BANK_BYTES)
+            for place in range(4):
+                q, h = tiles[place // 2]
+                staged[q, h, place % 2] = shared.tile([P, JH], F32, name="staged%d%d" % (n, place), align_bytes=64,
+                                                      offset=(n * 4 + place) * BANK_BYTES)
+
+        upper[0, 3] = shared.tile([P, 2, NQ, PACK], BF16, name="upper2", align_bytes=64, offset=8 * BANK_BYTES)
+        late = [shared.tile([P, JH], F32, name="late%d" % i, align_bytes=64, offset=(8 + i) * BANK_BYTES)
+                for i in range(NQ // P)]
+
+        def truncated(a, q):
+            return upper[a, q][:, 0] if (a, q) in upper else parts[a, q][:, 0]
+
+        def bank(number, shape, name):
+            return psum.tile(shape, F32, name=name, offset=number * BANK_BYTES)
+
+        banks = {(0, 1): (0, 1), (0, 0): (2, 3), (1, 1): (4, 5), (1, 0): (7, 6),
+                 (2, 0): (0, 1), (2, 1): (4, 5), (3, 0): (2, 3), (3, 1): (7, 6)}
         sums = {}
         turned = {}
 
@@ -75,9 +96,9 @@ def tile_list_tabts_gelu_kernel(tc, tab_words, tab_scales, w, ts, b, offs, out):
         def load_bias():
             rows = b.rearrange("(r p) -> r p", p=P).unsqueeze(0).to_broadcast([P * P // M, M // P, P])
             nc.sync.dma_start(out=bias_rows[:], in_=rows)
-            bank = psum.tile([P, P], F32, name="bank")
-            nc.tensor.transpose(bank[:], bias_rows[:], identity[:])
-            nc.scalar.copy(out=bias[:], in_=bank[:, :M // P])
+            turned_bias = bank(7, [P, P], "turned_bias")
+            nc.tensor.transpose(turned_bias[:], bias_rows[:], identity[:])
+            nc.scalar.copy(out=bias[:], in_=turned_bias[:, :M // P])
 
         def picks(h):
             return offsets[:, h * JH // 16:(h + 1) * JH // 16]
@@ -92,8 +113,8 @@ def tile_list_tabts_gelu_kernel(tc, tab_words, tab_scales, w, ts, b, offs, out):
             nc.vector.tensor_copy(ts_picked[h][:], ts_all[:].indirect(picks(h)))
 
         def truncate(a, q, copy=nc.scalar.copy):
-            upper = w_raw[a, q][:].bitcast(BF16).rearrange("p t (n i e) -> p n t i e", i=RUN, e=2)[:, :, :, :, 1]
-            copy(out=parts[a, q][:, 0].rearrange("p (n i) t -> p n t i", i=RUN), in_=upper)
+            halves = w_raw[a, q][:].bitcast(BF16).rearrange("p t (n i e) -> p n t i e", i=RUN, e=2)[:, :, :, :, 1]
+            copy(out=truncated(a, q).rearrange("p (n i) t -> p n t i", i=RUN), in_=halves)
 
         def weave(a, q):
             nc.scalar.copy(out=w_woven[a, q][:].rearrange("p (n i) t -> p n t i", i=RUN),
@@ -101,7 +122,8 @@ def tile_list_tabts_gelu_kernel(tc, tab_words, tab_scales, w, ts, b, offs, out):
 
         def mask(a, q, cols=slice(0, NQ)):
             pairs = parts[a, q][:, 0, cols].rearrange("p n t -> p (n t)").bitcast(I32)
-            nc.vector.tensor_scalar(pairs, pairs, HI_MASK, None, ALU.bitwise_and)
+            source = truncated(a, q)[:, cols].rearrange("p n t -> p (n t)").bitcast(I32)
+            nc.vector.tensor_scalar(pairs, source, HI_MASK, None, ALU.bitwise_and)
 
         def subtract(a, q, cols=slice(0, NQ)):
             nc.vector.tensor_tensor(parts[a, q][:, 1, cols].rearrange("p (n i) t -> p n t i", i=RUN),
@@ -122,7 +144,7 @@ def tile_list_tabts_gelu_kernel(tc, tab_words, tab_scales, w, ts, b, offs, out):
         def multiply(a, q, h):
             for i in range(NQ // P):
                 if a == 0:
-                    sums[q, h, i] = psum.tile([P, JH], F32, name="bank")
+                    sums[q, h, i] = bank(banks[q, h][i], [P, JH], "sum%d%d%d" % (q, h, i))
                 for s in range(2):
                     cols = slice(s * NQ + i * P, s * NQ + (i + 1) * P)
                     nc.tensor.matmul_mx(out=sums[q, h, i][:], lhsT=w_codes[a, q][:, cols].bitcast(FP8X4),
@@ -130,27 +152,28 @@ def tile_list_tabts_gelu_kernel(tc, tab_words, tab_scales, w, ts, b, offs, out):
                                         rhs_scale=v_scales[h][4 * a:, :],
                                         start=(a == 0 and s == 0), stop=(a == PASSES - 1 and s == 1))
 
-        def activate(source, q, i, cols, queue=nc.sync):
+        def activate(source, q, i, cols, queue=nc.sync, result=None):
             r = q * (NQ // P) + i
-            result = work.tile([P, cols.stop - cols.start], F32, name="result")
+            if result is None:
+                result = work.tile([P, cols.stop - cols.start], F32, name="result")
             nc.scalar.activation(result[:], source, ACT.Gelu_apprx_tanh, bias=bias[:, r:r + 1])
             queue.dma_start(out=out[r * P:(r + 1) * P, cols], in_=result[:])
 
         def finish(q, h, i, cols=slice(0, JH), queue=nc.sync):
-            scaled = work.tile([P, cols.stop - cols.start], F32, name="scaled")
-            nc.vector.tensor_tensor(scaled[:], sums[q, h, i][:, cols], ts_picked[h][:, cols], ALU.mult)
+            scaled = staged[q, h, i] if (q, h, i) in staged else work.tile([P, cols.stop - cols.start], F32, name="scaled")
+            nc.vector.tensor_tensor(scaled[:], ts_picked[h][:, cols], sums[q, h, i][:, cols], ALU.mult)
             activate(scaled[:], q, i, slice(h * JH + cols.start, h * JH + cols.stop), queue)
 
         def turn_ts():
-            bank = psum.tile([P, JH // P, P], F32, name="bank")
+            blocks = bank(6, [P, JH // P, P], "ts_blocks")
             for g in range(JH // P):
-                nc.tensor.transpose(bank[:, g, :], ts_picked[0][:, g * P:(g + 1) * P], identity[:])
-            nc.scalar.copy(out=ts_turned[:], in_=bank[:, :, 0])
+                nc.tensor.transpose(blocks[:, g, :], ts_picked[0][:, g * P:(g + 1) * P], identity[:])
+            nc.scalar.copy(out=ts_turned[:], in_=blocks[:, :, 0])
 
         def multiply_turned(q):
             for g in range(JH // P):
                 if g % 2 == 0:
-                    sums[q, 0, g // 2] = psum.tile([P, 2, NQ], F32, name="bank")
+                    sums[q, 0, g // 2] = bank(banks[q, 0][g // 2], [P, 2, NQ], "pair%d" % g)
                 entries = slice(g * P, (g + 1) * P)
                 for a in range(PASSES):
                     for s in range(2):
@@ -168,12 +191,12 @@ def tile_list_tabts_gelu_kernel(tc, tab_words, tab_scales, w, ts, b, offs, out):
                                      scale=ts_turned[:, g:g + 1])
 
         def finish_turned(q):
-            banks = [psum.tile([P, JH], F32, name="bank") for i in range(NQ // P)]
+            back = [bank(banks[q, 0][i], [P, JH], "back%d" % i) for i in range(NQ // P)]
             for i in range(NQ // P):
                 for g in range(JH // P):
-                    nc.tensor.transpose(banks[i][:, g * P:(g + 1) * P], turned[q][:, g, i * P:(i + 1) * P], identity[:])
+                    nc.tensor.transpose(back[i][:, g * P:(g + 1) * P], turned[q][:, g, i * P:(i + 1) * P], identity[:])
             for i in range(NQ // P):
-                activate(banks[i][:], q, i, slice(0, JH))
+                activate(back[i][:], q, i, slice(0, JH), result=late[i])
 
         nc.gpsimd.memset(table_scales[:, :T // 8], 0)
         nc.vector.memset(table_scales[:, T // 8:], 0)
@@ -198,7 +221,7 @@ def tile_list_tabts_gelu_kernel(tc, tab_words, tab_scales, w, ts, b, offs, out):
         for a, q in chunks[1:4]:
             truncate(a, q)
             weave(a, q)
-        for a, q in chunks[4:6]:
+        for a, q in chunks[4:7]:
             truncate(a, q)
 
         split_with_gpsimd(0, 0)
@@ -220,40 +243,42 @@ def tile_list_tabts_gelu_kernel(tc, tab_words, tab_scales, w, ts, b, offs, out):
         split_with_gpsimd(1, 1)
         gather_ts(0)
         turn_ts()
+        multiply(0, 1, 0)
+        weave(0, 2)
         scale_turned(0)
         gather_ts(1)
-        truncate(0, 3)
         quantize(1, 1)
-        multiply_turned(1)
         multiply(1, 1, 1)
-
-        mask(0, 2)
+        multiply(1, 1, 0)
+        split_with_gpsimd(0, 2)
         finish(0, 1, 0)
-        finish_turned(0)
-        scale_turned(1)
+        finish(0, 1, 1)
+        finish(1, 1, 0)
+        finish(1, 1, 1)
         truncate(1, 3)
-        subtract(0, 2)
+        weave(1, 3)
         mask(1, 2)
         quantize(0, 2)
         for h in range(HALVES):
             multiply(0, 2, h)
-        finish_turned(1)
         subtract(1, 2)
-        finish(0, 1, 1)
-        finish(1, 1, 0)
+        mask(0, 3)
+        finish_turned(0)
         quantize(1, 2)
         for h in range(HALVES):
             multiply(1, 2, h)
-        mask(0, 3)
-        mask(1, 3)
-        finish(1, 1, 1)
         subtract(0, 3)
-        finish(2, 0, 0)
+        mask(1, 3, slice(0, VECTOR_COLUMNS))
         quantize(0, 3)
-        for h in range(HALVES):
-            multiply(0, 3, h)
-        subtract(1, 3)
-        finish(2, 0, 1)
+        multiply(0, 3, 0)
+        subtract(1, 3, slice(0, VECTOR_COLUMNS))
+        rest = slice(VECTOR_COLUMNS, NQ)
+        mask(1, 3, rest)
+        nc.gpsimd.tensor_tensor(parts[1, 3][:, 1, rest], w_woven[1, 3][:], parts[1, 3][:, 0, rest], ALU.subtract)
+        for q in (1, 2):
+            for i in range(NQ // P):
+                finish(q, 0, i)
+        multiply(0, 3, 1)
         quantize(1, 3)
         for h in range(HALVES):
             multiply(1, 3, h)

@@ -25,65 +25,70 @@ JH = 512
 HALVES = S // JH
 RUN = 4
 HI_MASK = 0xFFF0FFF0 - (1 << 32)
-VECTOR_COLUMNS = NQ // 8
-STAGING_BUFS = 8
+RESULT_BUFS = 8
 BANK_BYTES = 4 * JH
+KB = 1024
 
 
 def tile_list_tabts_gelu_kernel(tc, tab_words, tab_scales, w, ts, b, offs, out):
     nc = tc.nc
     with ExitStack() as ctx:
         keep = ctx.enter_context(tc.tile_pool(name="keep", bufs=1))
-        work = ctx.enter_context(tc.tile_pool(name="work", bufs=STAGING_BUFS))
+        work = ctx.enter_context(tc.tile_pool(name="work", bufs=RESULT_BUFS))
         psum = ctx.enter_context(tc.psum_pool(name="psum", bufs=1))
-        shared = ctx.enter_context(tc.tile_pool(name="shared", bufs=1))
+        arena = ctx.enter_context(tc.tile_pool(name="arena", bufs=1))
 
         chunks = [(a, q) for q in range(QUARTERS) for a in range(PASSES)]
+        place = {
+            "w_late10": 0, "w_codes00": 0, "w_raw01": 4, "w_codes10": 4, "w_raw11": 8, "w_codes01": 8,
+            "w_raw02": 12, "w_codes11": 12, "w_raw12": 16, "w_codes02": 16,
+            "w_woven00": 24, "upper10": 28, "v_codes0": 26,
+            "w_woven10": 30, "upper01": 34, "v_codes1": 32,
+            "w_woven01": 36, "upper11": 40, "ts_picked": 38,
+            "w_woven11": 50, "upper02": 54, "staged0": 50,
+            "w_woven02": 60, "upper12": 64, "staged1": 62,
+            "upper13": 78, "staged2": 78,
+        }
+
+        def sbuf(name, shape, dtype):
+            if name in place:
+                return arena.tile(shape, dtype, name=name, align_bytes=64, offset=place[name] * KB)
+            return keep.tile(shape, dtype, name=name, align_bytes=64)
+
         offsets = keep.tile([P, S // 16], U16, name="offsets")
-        table_words = [keep.tile([P, T], I32, name="table_words%d" % a, align_bytes=64) for a in range(PASSES)]
-        table_scales = keep.tile([P, T // 4], I32, name="table_scales", align_bytes=64)
-        ts_all = keep.tile([P, T], F32, name="ts_all", align_bytes=64)
-        bias_rows = keep.tile([P, P], F32, name="bias_rows")
-        bias = keep.tile([P, M // P], F32, name="bias")
-        warm = keep.tile([P, 8], F32, name="warm")
-        identity = keep.tile([P, P], F32, name="identity")
-        w_raw = {c: keep.tile([P, PACK, NQ], F32, name="w_raw%d%d" % c, align_bytes=64) for c in chunks}
-        parts = {c: keep.tile([P, 2, NQ, PACK], BF16, name="parts%d%d" % c, align_bytes=64) for c in chunks}
-        w_woven = {c: keep.tile([P, NQ - VECTOR_COLUMNS, PACK], F32, name="w_woven%d%d" % c, align_bytes=64)
-                   for c in chunks[:5] + chunks[7:]}
-        w_codes = {c: keep.tile([P, 2 * NQ], U32, name="w_codes%d%d" % c, align_bytes=64) for c in chunks}
-        w_scales = {c: keep.tile([P, 2 * NQ], U8, name="w_scales%d%d" % c, align_bytes=64) for c in chunks}
-        v_codes = {(a, h): keep.tile([P, JH], U32, name="v_codes%d%d" % (a, h), align_bytes=64)
-                   for a in range(PASSES) for h in range(HALVES)}
-        v_scales = [keep.tile([P, JH], U8, name="v_scales%d" % h, align_bytes=64) for h in range(HALVES)]
-        ts_picked = [keep.tile([P, JH], F32, name="ts_picked%d" % h, align_bytes=64) for h in range(HALVES)]
-        ts_turned = keep.tile([P, JH // P], F32, name="ts_turned")
-        upper, staged = {}, {}
-        for n, (c, tiles) in enumerate((((0, 2), ((0, 1), (1, 1))), ((1, 3), ((1, 0), (2, 0))))):
-            upper[c] = shared.tile([P, 4, NQ, PACK], BF16, name="upper%d" % n, align_bytes=64, offset=n * 4 * BANK_BYTES)
-            for place in range(4):
-                q, h = tiles[place // 2]
-                staged[q, h, place % 2] = shared.tile([P, JH], F32, name="staged%d%d" % (n, place), align_bytes=64,
-                                                      offset=(n * 4 + place) * BANK_BYTES)
-
-        upper[0, 3] = shared.tile([P, 2, NQ, PACK], BF16, name="upper2", align_bytes=64, offset=8 * BANK_BYTES)
-        late = [shared.tile([P, JH], F32, name="late%d" % i, align_bytes=64, offset=(8 + i) * BANK_BYTES)
-                for i in range(NQ // P)]
-
-        def truncated(a, q):
-            return upper[a, q][:, 0] if (a, q) in upper else parts[a, q][:, 0]
+        table_words = [sbuf("table_words%d" % a, [P, T], I32) for a in range(PASSES)]
+        table_scales = sbuf("table_scales", [P, T // 4], I32)
+        ts_all = sbuf("ts_all", [P, T], F32)
+        bias_rows = sbuf("bias_rows", [P, P], F32)
+        bias = sbuf("bias", [P, M // P], F32)
+        warm = sbuf("warm", [P, 8], F32)
+        identity = sbuf("identity", [P, P], F32)
+        woven_chunks = [c for c in chunks if c != (0, 3)]
+        w_raw = {c: [sbuf("w_raw%d%d" % c, [P, PACK, NQ], F32)] for c in chunks if c != (1, 0)}
+        w_raw[1, 0] = [sbuf(name, [P, PACK, NQ // 2], F32) for name in ("w_early10", "w_late10")]
+        upper = {c: sbuf("upper%d%d" % c, [P, NQ, PACK], BF16) for c in chunks}
+        parts = {c: sbuf("parts%d%d" % c, [P, 2, NQ, PACK], BF16) for c in chunks}
+        w_woven = {c: sbuf("w_woven%d%d" % c, [P, NQ, PACK], F32) for c in woven_chunks}
+        w_codes = {c: sbuf("w_codes%d%d" % c, [P, 2 * NQ], U32) for c in chunks}
+        w_scales = {c: sbuf("w_scales%d%d" % c, [P, 2 * NQ], U8) for c in chunks}
+        v_codes = [sbuf("v_codes%d" % a, [P, S], U32) for a in range(PASSES)]
+        v_scales = sbuf("v_scales", [P, S], U8)
+        ts_picked = sbuf("ts_picked", [P, S], F32)
+        staged = [sbuf("staged%d" % q, [P, 4, JH], F32) for q in range(QUARTERS)]
 
         def bank(number, shape, name):
             return psum.tile(shape, F32, name=name, offset=number * BANK_BYTES)
 
-        banks = {(0, 1): (0, 1), (0, 0): (2, 3), (1, 1): (4, 5), (1, 0): (7, 6),
-                 (2, 0): (0, 1), (2, 1): (4, 5), (3, 0): (2, 3), (3, 1): (7, 6)}
         sums = {}
-        turned = {}
+
+        def pieces(a, q):
+            width = NQ // len(w_raw[a, q])
+            return [(raw, slice(n * width, (n + 1) * width)) for n, raw in enumerate(w_raw[a, q])]
 
         def load_w(a, q):
-            rows = w[a * P * PACK:(a + 1) * P * PACK, q * NQ:(q + 1) * NQ]
-            nc.sync.dma_start(out=w_raw[a, q][:], in_=rows.rearrange("(p t) n -> p t n", t=PACK))
+            rows = w[a * P * PACK:(a + 1) * P * PACK, q * NQ:(q + 1) * NQ].rearrange("(p t) n -> p t n", t=PACK)
+            for raw, cols in pieces(a, q):
+                nc.sync.dma_start(out=raw[:], in_=rows[:, :, cols])
 
         def load_words(a):
             nc.sync.dma_start(out=table_words[a][:], in_=tab_words[a].rearrange("p t i -> p (t i)").bitcast(I32))
@@ -94,198 +99,162 @@ def tile_list_tabts_gelu_kernel(tc, tab_words, tab_scales, w, ts, b, offs, out):
                                   in_=tab_scales[:, 4 * quad:4 * quad + 4, :].bitcast(I32))
 
         def load_bias():
-            rows = b.rearrange("(r p) -> r p", p=P).unsqueeze(0).to_broadcast([P * P // M, M // P, P])
-            nc.sync.dma_start(out=bias_rows[:], in_=rows)
-            turned_bias = bank(7, [P, P], "turned_bias")
+            nc.sync.dma_start(out=bias_rows[:M // P, :], in_=b.rearrange("(r p) -> r p", p=P))
+
+        def turn_bias():
+            turned_bias = bank(3, [P, P], "turned_bias")
             nc.tensor.transpose(turned_bias[:], bias_rows[:], identity[:])
             nc.scalar.copy(out=bias[:], in_=turned_bias[:, :M // P])
+
+        def half(h):
+            return slice(h * JH, (h + 1) * JH)
 
         def picks(h):
             return offsets[:, h * JH // 16:(h + 1) * JH // 16]
 
         def gather_words(a, h):
-            nc.vector.tensor_copy(v_codes[a, h][:], table_words[a][:].bitcast(U32).indirect(picks(h)))
-
-        def gather_scales(h):
-            nc.vector.tensor_copy(v_scales[h][:], table_scales[:].bitcast(U8).indirect(picks(h)))
-
-        def gather_ts(h):
-            nc.vector.tensor_copy(ts_picked[h][:], ts_all[:].indirect(picks(h)))
+            nc.vector.tensor_copy(v_codes[a][:, half(h)], table_words[a][:].bitcast(U32).indirect(picks(h)))
 
         def truncate(a, q, copy=nc.scalar.copy):
-            halves = w_raw[a, q][:].bitcast(BF16).rearrange("p t (n i e) -> p n t i e", i=RUN, e=2)[:, :, :, :, 1]
-            copy(out=truncated(a, q).rearrange("p (n i) t -> p n t i", i=RUN), in_=halves)
+            for raw, cols in pieces(a, q):
+                if (a, q) in w_woven:
+                    nc.scalar.copy(out=w_woven[a, q][:, cols].rearrange("p (n i) t -> p n t i", i=RUN),
+                                   in_=raw[:].rearrange("p t (n i) -> p n t i", i=RUN))
+                halves = raw[:].bitcast(BF16).rearrange("p t (n i e) -> p n t i e", i=RUN, e=2)[:, :, :, :, 1]
+                copy(out=upper[a, q][:, cols].rearrange("p (n i) t -> p n t i", i=RUN), in_=halves)
 
-        def weave(a, q):
-            nc.scalar.copy(out=w_woven[a, q][:].rearrange("p (n i) t -> p n t i", i=RUN),
-                           in_=w_raw[a, q][:, :, VECTOR_COLUMNS:].rearrange("p t (n i) -> p n t i", i=RUN))
-
-        def mask(a, q, cols=slice(0, NQ)):
-            pairs = parts[a, q][:, 0, cols].rearrange("p n t -> p (n t)").bitcast(I32)
-            source = truncated(a, q)[:, cols].rearrange("p n t -> p (n t)").bitcast(I32)
+        def mask(a, q):
+            pairs = parts[a, q][:, 0].rearrange("p n t -> p (n t)").bitcast(I32)
+            source = upper[a, q][:].rearrange("p n t -> p (n t)").bitcast(I32)
             nc.vector.tensor_scalar(pairs, source, HI_MASK, None, ALU.bitwise_and)
 
-        def subtract(a, q, cols=slice(0, NQ)):
-            nc.vector.tensor_tensor(parts[a, q][:, 1, cols].rearrange("p (n i) t -> p n t i", i=RUN),
-                                    w_raw[a, q][:, :, cols].rearrange("p t (n i) -> p n t i", i=RUN),
-                                    parts[a, q][:, 0, cols].rearrange("p (n i) t -> p n t i", i=RUN), ALU.subtract)
+        def subtract(a, q):
+            nc.vector.tensor_tensor(parts[a, q][:, 1].rearrange("p (n i) t -> p n t i", i=RUN),
+                                    w_raw[a, q][0][:].rearrange("p t (n i) -> p n t i", i=RUN),
+                                    parts[a, q][:, 0].rearrange("p (n i) t -> p n t i", i=RUN), ALU.subtract)
 
-        def split_with_gpsimd(a, q):
-            own, rest = slice(0, VECTOR_COLUMNS), slice(VECTOR_COLUMNS, NQ)
-            mask(a, q, own)
-            mask(a, q, rest)
-            subtract(a, q, own)
-            nc.gpsimd.tensor_tensor(parts[a, q][:, 1, rest], w_woven[a, q][:], parts[a, q][:, 0, rest], ALU.subtract)
+        def subtract_on_gpsimd(a, q):
+            nc.gpsimd.tensor_tensor(parts[a, q][:, 1], w_woven[a, q][:], parts[a, q][:, 0], ALU.subtract)
 
-        def quantize(a, q):
-            nc.vector.quantize_mx(out=w_codes[a, q][:].bitcast(FP8X4), scales=w_scales[a, q][:],
-                                  in_=parts[a, q][:].rearrange("p s n t -> p (s n t)"))
+        def quantize(a, q, first=0, last=2):
+            cols = slice(first * NQ, last * NQ)
+            nc.vector.quantize_mx(out=w_codes[a, q][:, cols].bitcast(FP8X4), scales=w_scales[a, q][:, cols],
+                                  in_=parts[a, q][:, first:last].rearrange("p s n t -> p (s n t)"))
 
-        def multiply(a, q, h):
-            for i in range(NQ // P):
-                if a == 0:
-                    sums[q, h, i] = bank(banks[q, h][i], [P, JH], "sum%d%d%d" % (q, h, i))
-                for s in range(2):
-                    cols = slice(s * NQ + i * P, s * NQ + (i + 1) * P)
-                    nc.tensor.matmul_mx(out=sums[q, h, i][:], lhsT=w_codes[a, q][:, cols].bitcast(FP8X4),
-                                        lhsT_scale=w_scales[a, q][:, cols], rhs=v_codes[a, h][:].bitcast(FP8X4),
-                                        rhs_scale=v_scales[h][4 * a:, :],
-                                        start=(a == 0 and s == 0), stop=(a == PASSES - 1 and s == 1))
-
-        def activate(source, q, i, cols, queue=nc.sync, result=None):
-            r = q * (NQ // P) + i
-            if result is None:
-                result = work.tile([P, cols.stop - cols.start], F32, name="result")
-            nc.scalar.activation(result[:], source, ACT.Gelu_apprx_tanh, bias=bias[:, r:r + 1])
-            queue.dma_start(out=out[r * P:(r + 1) * P, cols], in_=result[:])
-
-        def finish(q, h, i, cols=slice(0, JH), queue=nc.sync):
-            scaled = staged[q, h, i] if (q, h, i) in staged else work.tile([P, cols.stop - cols.start], F32, name="scaled")
-            nc.vector.tensor_tensor(scaled[:], ts_picked[h][:, cols], sums[q, h, i][:, cols], ALU.mult)
-            activate(scaled[:], q, i, slice(h * JH + cols.start, h * JH + cols.stop), queue)
-
-        def turn_ts():
-            blocks = bank(6, [P, JH // P, P], "ts_blocks")
-            for g in range(JH // P):
-                nc.tensor.transpose(blocks[:, g, :], ts_picked[0][:, g * P:(g + 1) * P], identity[:])
-            nc.scalar.copy(out=ts_turned[:], in_=blocks[:, :, 0])
-
-        def multiply_turned(q):
-            for g in range(JH // P):
-                if g % 2 == 0:
-                    sums[q, 0, g // 2] = bank(banks[q, 0][g // 2], [P, 2, NQ], "pair%d" % g)
-                entries = slice(g * P, (g + 1) * P)
-                for a in range(PASSES):
-                    for s in range(2):
-                        cols = slice(s * NQ, (s + 1) * NQ)
-                        nc.tensor.matmul_mx(out=sums[q, 0, g // 2][:, g % 2, :],
-                                            lhsT=v_codes[a, 0][:, entries].bitcast(FP8X4),
-                                            lhsT_scale=v_scales[0][4 * a:, entries],
-                                            rhs=w_codes[a, q][:, cols].bitcast(FP8X4), rhs_scale=w_scales[a, q][:, cols],
+        def multiply(a, q, first=0, last=2):
+            for h in range(HALVES):
+                for i in range(NQ // P):
+                    if a == 0 and first == 0:
+                        sums[q, h, i] = bank(4 * (q % 2) + 2 * h + i, [P, JH], "sum%d%d%d" % (q, h, i))
+                    for s in range(first, last):
+                        cols = slice(s * NQ + i * P, s * NQ + (i + 1) * P)
+                        nc.tensor.matmul_mx(out=sums[q, h, i][:], lhsT=w_codes[a, q][:, cols].bitcast(FP8X4),
+                                            lhsT_scale=w_scales[a, q][:, cols],
+                                            rhs=v_codes[a][:, half(h)].bitcast(FP8X4),
+                                            rhs_scale=v_scales[4 * a:, half(h)],
                                             start=(a == 0 and s == 0), stop=(a == PASSES - 1 and s == 1))
 
-        def scale_turned(q):
-            turned[q] = keep.tile([P, JH // P, NQ], F32, name="turned%d" % q)
-            for g in range(JH // P):
-                nc.scalar.activation(turned[q][:, g, :], sums[q, 0, g // 2][:, g % 2, :], ACT.Copy,
-                                     scale=ts_turned[:, g:g + 1])
+        def scale(q, h, i, cols=slice(0, JH)):
+            nc.vector.tensor_tensor(staged[q][:, 2 * h + i, cols], ts_picked[:, h * JH + cols.start:h * JH + cols.stop], sums[q, h, i][:, cols],
+                                    ALU.mult)
 
-        def finish_turned(q):
-            back = [bank(banks[q, 0][i], [P, JH], "back%d" % i) for i in range(NQ // P)]
-            for i in range(NQ // P):
-                for g in range(JH // P):
-                    nc.tensor.transpose(back[i][:, g * P:(g + 1) * P], turned[q][:, g, i * P:(i + 1) * P], identity[:])
-            for i in range(NQ // P):
-                activate(back[i][:], q, i, slice(0, JH), result=late[i])
+        def activate(q, h, i, cols=slice(0, JH), queue=nc.sync):
+            r = q * (NQ // P) + i
+            result = work.tile([P, cols.stop - cols.start], F32, name="result")
+            nc.scalar.activation(result[:], staged[q][:, 2 * h + i, cols], ACT.Gelu_apprx_tanh, bias=bias[:, r:r + 1])
+            queue.dma_start(out=out[r * P:(r + 1) * P, h * JH + cols.start:h * JH + cols.stop], in_=result[:])
+
+        def scale_quarter(q):
+            for h in range(HALVES):
+                for i in range(NQ // P):
+                    scale(q, h, i)
+
+        def activate_quarter(q):
+            for h in range(HALVES):
+                for i in range(NQ // P):
+                    activate(q, h, i)
 
         nc.gpsimd.memset(table_scales[:, :T // 8], 0)
         nc.vector.memset(table_scales[:, T // 8:], 0)
         nc.gpsimd.memset(warm[:], 0.0)
         nc.scalar.activation(warm[:, 4:5], warm[:, 0:1], ACT.Gelu_apprx_tanh)
+        nc.gpsimd.memset(bias_rows[:], 0.0)
         make_identity(nc, identity[:])
 
         nc.sync.dma_start(offsets[:], offs)
         load_w(0, 0)
         load_scales()
-        load_bias()
         load_w(1, 0)
         load_words(0)
+        load_bias()
         load_w(0, 1)
         load_words(1)
         load_w(1, 1)
         nc.sync.dma_start(out=ts_all[:], in_=ts)
         for a, q in chunks[4:]:
             load_w(a, q)
+        turn_bias()
+
         truncate(0, 0, nc.vector.tensor_copy)
-        weave(0, 0)
         for a, q in chunks[1:4]:
             truncate(a, q)
-            weave(a, q)
-        for a, q in chunks[4:7]:
-            truncate(a, q)
-
-        split_with_gpsimd(0, 0)
-        gather_scales(1)
-        gather_scales(0)
+        mask(0, 0)
+        subtract_on_gpsimd(0, 0)
+        nc.vector.tensor_copy(v_scales[:], table_scales[:].bitcast(U8).indirect(offsets[:]))
+        mask(1, 0)
+        subtract_on_gpsimd(1, 0)
         quantize(0, 0)
-        split_with_gpsimd(1, 0)
-        gather_words(0, 1)
-        multiply(0, 0, 1)
         gather_words(0, 0)
+        gather_words(0, 1)
+        multiply(0, 0)
+        mask(0, 1)
+        subtract_on_gpsimd(0, 1)
         quantize(1, 0)
-        split_with_gpsimd(0, 1)
         gather_words(1, 0)
-        multiply_turned(0)
         gather_words(1, 1)
-        multiply(1, 0, 1)
+        multiply(1, 0)
+        mask(1, 1)
+        subtract_on_gpsimd(1, 1)
         quantize(0, 1)
-        multiply(0, 1, 1)
-        split_with_gpsimd(1, 1)
-        gather_ts(0)
-        turn_ts()
-        multiply(0, 1, 0)
-        weave(0, 2)
-        scale_turned(0)
-        gather_ts(1)
+        nc.vector.tensor_copy(ts_picked[:], ts_all[:].indirect(offsets[:]))
+        multiply(0, 1)
+        truncate(0, 2)
+        truncate(1, 2)
+        mask(0, 2)
+        subtract_on_gpsimd(0, 2)
         quantize(1, 1)
-        multiply(1, 1, 1)
-        multiply(1, 1, 0)
-        split_with_gpsimd(0, 2)
-        finish(0, 1, 0)
-        finish(0, 1, 1)
-        finish(1, 1, 0)
-        finish(1, 1, 1)
+        multiply(1, 1)
+        scale_quarter(0)
+        activate_quarter(0)
+        truncate(0, 3)
         truncate(1, 3)
-        weave(1, 3)
         mask(1, 2)
+        subtract_on_gpsimd(1, 2)
         quantize(0, 2)
-        for h in range(HALVES):
-            multiply(0, 2, h)
-        subtract(1, 2)
+        multiply(0, 2)
+        quantize(1, 2, 0, 1)
+        multiply(1, 2, 0, 1)
+        scale_quarter(1)
+        activate_quarter(1)
         mask(0, 3)
-        finish_turned(0)
-        quantize(1, 2)
-        for h in range(HALVES):
-            multiply(1, 2, h)
+        quantize(1, 2, 1, 2)
+        multiply(1, 2, 1, 2)
+        quantize(0, 3, 0, 1)
+        multiply(0, 3, 0, 1)
         subtract(0, 3)
-        mask(1, 3, slice(0, VECTOR_COLUMNS))
-        quantize(0, 3)
-        multiply(0, 3, 0)
-        subtract(1, 3, slice(0, VECTOR_COLUMNS))
-        rest = slice(VECTOR_COLUMNS, NQ)
-        mask(1, 3, rest)
-        nc.gpsimd.tensor_tensor(parts[1, 3][:, 1, rest], w_woven[1, 3][:], parts[1, 3][:, 0, rest], ALU.subtract)
-        for q in (1, 2):
-            for i in range(NQ // P):
-                finish(q, 0, i)
-        multiply(0, 3, 1)
-        quantize(1, 3)
-        for h in range(HALVES):
-            multiply(1, 3, h)
-        finish(2, 1, 0)
-        finish(2, 1, 1)
-        finish(3, 0, 0)
-        finish(3, 0, 1)
-        finish(3, 1, 0)
-        finish(3, 1, 1, slice(0, JH // 2))
-        finish(3, 1, 1, slice(JH // 2, JH), nc.scalar)
+        mask(1, 3)
+        subtract_on_gpsimd(1, 3)
+        quantize(0, 3, 1, 2)
+        multiply(0, 3, 1, 2)
+        quantize(1, 3, 0, 1)
+        multiply(1, 3, 0, 1)
+        scale_quarter(2)
+        activate_quarter(2)
+        quantize(1, 3, 1, 2)
+        multiply(1, 3, 1, 2)
+        for h, i in ((0, 0), (0, 1), (1, 0)):
+            scale(3, h, i)
+            activate(3, h, i)
+        for cols, queue in ((slice(0, JH // 2), nc.sync), (slice(JH // 2, JH), nc.scalar)):
+            scale(3, 1, 1, cols)
+            activate(3, 1, 1, cols, queue)

@@ -28,6 +28,7 @@ HI_MASK = 0xFFF0FFF0 - (1 << 32)
 RESULT_BUFS = 8
 BANK_BYTES = 4 * JH
 KB = 1024
+VECTOR_COLUMNS = NQ // 8
 
 
 def tile_list_tabts_gelu_kernel(tc, tab_words, tab_scales, w, ts, b, offs, out):
@@ -40,7 +41,7 @@ def tile_list_tabts_gelu_kernel(tc, tab_words, tab_scales, w, ts, b, offs, out):
 
         chunks = [(a, q) for q in range(QUARTERS) for a in range(PASSES)]
         place = {
-            "w_late10": 0, "w_codes00": 0, "w_raw01": 4, "w_codes10": 4, "w_raw11": 8, "w_codes01": 8,
+            "w_raw10": 0, "w_codes00": 0, "w_raw01": 4, "w_codes10": 4, "w_raw11": 8, "w_codes01": 8,
             "w_raw02": 12, "w_codes11": 12, "w_raw12": 16, "w_codes02": 16,
             "w_woven00": 24, "upper10": 28, "v_codes0": 26,
             "w_woven10": 30, "upper01": 34, "v_codes1": 32,
@@ -64,8 +65,7 @@ def tile_list_tabts_gelu_kernel(tc, tab_words, tab_scales, w, ts, b, offs, out):
         warm = sbuf("warm", [P, 8], F32)
         identity = sbuf("identity", [P, P], F32)
         woven_chunks = [c for c in chunks if c != (0, 3)]
-        w_raw = {c: [sbuf("w_raw%d%d" % c, [P, PACK, NQ], F32)] for c in chunks if c != (1, 0)}
-        w_raw[1, 0] = [sbuf(name, [P, PACK, NQ // 2], F32) for name in ("w_early10", "w_late10")]
+        w_raw = {c: [sbuf("w_raw%d%d" % c, [P, PACK, NQ], F32)] for c in chunks}
         upper = {c: sbuf("upper%d%d" % c, [P, NQ, PACK], BF16) for c in chunks}
         parts = {c: sbuf("parts%d%d" % c, [P, 2, NQ, PACK], BF16) for c in chunks}
         w_woven = {c: sbuf("w_woven%d%d" % c, [P, NQ, PACK], F32) for c in woven_chunks}
@@ -123,18 +123,23 @@ def tile_list_tabts_gelu_kernel(tc, tab_words, tab_scales, w, ts, b, offs, out):
                 halves = raw[:].bitcast(BF16).rearrange("p t (n i e) -> p n t i e", i=RUN, e=2)[:, :, :, :, 1]
                 copy(out=upper[a, q][:, cols].rearrange("p (n i) t -> p n t i", i=RUN), in_=halves)
 
-        def mask(a, q):
-            pairs = parts[a, q][:, 0].rearrange("p n t -> p (n t)").bitcast(I32)
-            source = upper[a, q][:].rearrange("p n t -> p (n t)").bitcast(I32)
+        def mask(a, q, cols=slice(0, NQ)):
+            pairs = parts[a, q][:, 0, cols].rearrange("p n t -> p (n t)").bitcast(I32)
+            source = upper[a, q][:, cols].rearrange("p n t -> p (n t)").bitcast(I32)
             nc.vector.tensor_scalar(pairs, source, HI_MASK, None, ALU.bitwise_and)
 
-        def subtract(a, q):
-            nc.vector.tensor_tensor(parts[a, q][:, 1].rearrange("p (n i) t -> p n t i", i=RUN),
-                                    w_raw[a, q][0][:].rearrange("p t (n i) -> p n t i", i=RUN),
-                                    parts[a, q][:, 0].rearrange("p (n i) t -> p n t i", i=RUN), ALU.subtract)
+        def subtract(a, q, cols=slice(0, NQ)):
+            nc.vector.tensor_tensor(parts[a, q][:, 1, cols].rearrange("p (n i) t -> p n t i", i=RUN),
+                                    w_raw[a, q][0][:, :, cols].rearrange("p t (n i) -> p n t i", i=RUN),
+                                    parts[a, q][:, 0, cols].rearrange("p (n i) t -> p n t i", i=RUN), ALU.subtract)
 
         def subtract_on_gpsimd(a, q):
-            nc.gpsimd.tensor_tensor(parts[a, q][:, 1], w_woven[a, q][:], parts[a, q][:, 0], ALU.subtract)
+            rest = slice(VECTOR_COLUMNS, NQ)
+            nc.gpsimd.tensor_tensor(parts[a, q][:, 1, rest], w_woven[a, q][:, rest], parts[a, q][:, 0, rest], ALU.subtract)
+
+        def subtract_share(a, q):
+            own = slice(0, VECTOR_COLUMNS)
+            nc.vector.tensor_tensor(parts[a, q][:, 1, own], w_woven[a, q][:, own], parts[a, q][:, 0, own], ALU.subtract)
 
         def quantize(a, q, first=0, last=2):
             cols = slice(first * NQ, last * NQ)
@@ -198,24 +203,29 @@ def tile_list_tabts_gelu_kernel(tc, tab_words, tab_scales, w, ts, b, offs, out):
         truncate(0, 0, nc.vector.tensor_copy)
         for a, q in chunks[1:4]:
             truncate(a, q)
-        mask(0, 0)
+        mask(0, 0, slice(0, VECTOR_COLUMNS))
+        mask(0, 0, slice(VECTOR_COLUMNS, NQ))
+        subtract(0, 0, slice(0, VECTOR_COLUMNS))
         subtract_on_gpsimd(0, 0)
         nc.vector.tensor_copy(v_scales[:], table_scales[:].bitcast(U8).indirect(offsets[:]))
         mask(1, 0)
         subtract_on_gpsimd(1, 0)
         quantize(0, 0)
+        subtract_share(1, 0)
         gather_words(0, 0)
         gather_words(0, 1)
         multiply(0, 0)
         mask(0, 1)
         subtract_on_gpsimd(0, 1)
         quantize(1, 0)
+        subtract_share(0, 1)
         gather_words(1, 0)
         gather_words(1, 1)
         multiply(1, 0)
         mask(1, 1)
         subtract_on_gpsimd(1, 1)
         quantize(0, 1)
+        subtract_share(1, 1)
         nc.vector.tensor_copy(ts_picked[:], ts_all[:].indirect(offsets[:]))
         multiply(0, 1)
         truncate(0, 2)
@@ -223,6 +233,7 @@ def tile_list_tabts_gelu_kernel(tc, tab_words, tab_scales, w, ts, b, offs, out):
         mask(0, 2)
         subtract_on_gpsimd(0, 2)
         quantize(1, 1)
+        subtract_share(0, 2)
         multiply(1, 1)
         scale_quarter(0)
         activate_quarter(0)
@@ -231,6 +242,7 @@ def tile_list_tabts_gelu_kernel(tc, tab_words, tab_scales, w, ts, b, offs, out):
         mask(1, 2)
         subtract_on_gpsimd(1, 2)
         quantize(0, 2)
+        subtract_share(1, 2)
         multiply(0, 2)
         quantize(1, 2, 0, 1)
         multiply(1, 2, 0, 1)
@@ -245,6 +257,7 @@ def tile_list_tabts_gelu_kernel(tc, tab_words, tab_scales, w, ts, b, offs, out):
         mask(1, 3)
         subtract_on_gpsimd(1, 3)
         quantize(0, 3, 1, 2)
+        subtract_share(1, 3)
         multiply(0, 3, 1, 2)
         quantize(1, 3, 0, 1)
         multiply(1, 3, 0, 1)

@@ -28,7 +28,8 @@ HI_MASK = 0xFFF0FFF0 - (1 << 32)
 RESULT_BUFS = 8
 BANK_BYTES = 4 * JH
 KB = 1024
-VECTOR_COLUMNS = NQ // 8
+WOVEN_SHARE = NQ // 8
+PLAIN_SHARE = NQ // 4
 
 
 def tile_list_tabts_gelu_kernel(tc, tab_words, tab_scales, w, ts, b, offs, out):
@@ -41,14 +42,10 @@ def tile_list_tabts_gelu_kernel(tc, tab_words, tab_scales, w, ts, b, offs, out):
 
         chunks = [(a, q) for q in range(QUARTERS) for a in range(PASSES)]
         place = {
-            "w_raw10": 0, "w_codes00": 0, "w_raw01": 4, "w_codes10": 4, "w_raw11": 8, "w_codes01": 8,
-            "w_raw02": 12, "w_codes11": 12, "w_raw12": 16, "w_codes02": 16,
-            "w_woven00": 24, "upper10": 28, "v_codes0": 26,
-            "w_woven10": 30, "upper01": 34, "v_codes1": 32,
-            "w_woven01": 36, "upper11": 40, "ts_picked": 38,
-            "w_woven11": 50, "upper02": 54, "staged0": 50,
-            "w_woven02": 60, "upper12": 64, "staged1": 62,
-            "upper13": 78, "staged2": 78,
+            "upper02": 0, "staged0": 0,
+            "parts12": 10, "w_raw02": 12,
+            "upper03": 16, "staged1": 16,
+            "parts13": 24, "w_raw03": 26,
         }
 
         def sbuf(name, shape, dtype):
@@ -64,9 +61,9 @@ def tile_list_tabts_gelu_kernel(tc, tab_words, tab_scales, w, ts, b, offs, out):
         bias = sbuf("bias", [P, M // P], F32)
         warm = sbuf("warm", [P, 8], F32)
         identity = sbuf("identity", [P, P], F32)
-        woven_chunks = [c for c in chunks if c != (0, 3)]
+        woven_chunks = chunks[:4]
         w_raw = {c: [sbuf("w_raw%d%d" % c, [P, PACK, NQ], F32)] for c in chunks}
-        upper = {c: sbuf("upper%d%d" % c, [P, NQ, PACK], BF16) for c in chunks}
+        upper = {c: sbuf("upper%d%d" % c, [P, 1, NQ, PACK], BF16)[:, 0] for c in chunks}
         parts = {c: sbuf("parts%d%d" % c, [P, 2, NQ, PACK], BF16) for c in chunks}
         w_woven = {c: sbuf("w_woven%d%d" % c, [P, NQ, PACK], F32) for c in woven_chunks}
         w_codes = {c: sbuf("w_codes%d%d" % c, [P, 2 * NQ], U32) for c in chunks}
@@ -74,7 +71,15 @@ def tile_list_tabts_gelu_kernel(tc, tab_words, tab_scales, w, ts, b, offs, out):
         v_codes = [sbuf("v_codes%d" % a, [P, S], U32) for a in range(PASSES)]
         v_scales = sbuf("v_scales", [P, S], U8)
         ts_picked = sbuf("ts_picked", [P, S], F32)
-        staged = [sbuf("staged%d" % q, [P, 4, JH], F32) for q in range(QUARTERS)]
+        groups = [[(0, 1), (1, 0)], [(1, 1), (2, 0)], [(2, 1), (3, 0)], [(3, 1)]]
+        staged = {}
+        for n, tiles in enumerate(groups):
+            area = sbuf("staged%d" % n, [P, 2 * len(tiles), JH], F32)
+            for m, (q, h) in enumerate(tiles):
+                for i in range(NQ // P):
+                    staged[q, h, i] = area[:, 2 * m + i]
+        ts_column = sbuf("ts_column", [P, JH // P], F32)
+        turned = [sbuf("turned%d" % q, [P, JH // P, NQ], F32) for q in range(2)]
 
         def bank(number, shape, name):
             return psum.tile(shape, F32, name=name, offset=number * BANK_BYTES)
@@ -115,13 +120,29 @@ def tile_list_tabts_gelu_kernel(tc, tab_words, tab_scales, w, ts, b, offs, out):
         def gather_words(a, h):
             nc.vector.tensor_copy(v_codes[a][:, half(h)], table_words[a][:].bitcast(U32).indirect(picks(h)))
 
+        def share(a, q):
+            return WOVEN_SHARE if (a, q) in w_woven else PLAIN_SHARE
+
         def truncate(a, q, copy=nc.scalar.copy):
-            for raw, cols in pieces(a, q):
-                if (a, q) in w_woven:
-                    nc.scalar.copy(out=w_woven[a, q][:, cols].rearrange("p (n i) t -> p n t i", i=RUN),
-                                   in_=raw[:].rearrange("p t (n i) -> p n t i", i=RUN))
-                halves = raw[:].bitcast(BF16).rearrange("p t (n i e) -> p n t i e", i=RUN, e=2)[:, :, :, :, 1]
-                copy(out=upper[a, q][:, cols].rearrange("p (n i) t -> p n t i", i=RUN), in_=halves)
+            halves = w_raw[a, q][0][:].bitcast(BF16).rearrange("p t (n i e) -> p n t i e", i=RUN, e=2)[:, :, :, :, 1]
+            copy(out=upper[a, q].rearrange("p (n i) t -> p n t i", i=RUN), in_=halves)
+
+        def weave(a, q):
+            cols = slice(share(a, q), NQ)
+            nc.scalar.copy(out=w_woven[a, q][:, cols].rearrange("p (n i) t -> p n t i", i=RUN),
+                           in_=w_raw[a, q][0][:, :, cols].rearrange("p t (n i) -> p n t i", i=RUN))
+
+        def split(a, q):
+            own, rest = slice(0, share(a, q)), slice(share(a, q), NQ)
+            mask(a, q, own)
+            mask(a, q, rest)
+            subtract(a, q, own)
+            subtract_rest(a, q)
+
+        def subtract_rest(a, q):
+            rest = slice(share(a, q), NQ)
+            source = w_woven[a, q][:] if (a, q) in w_woven else w_raw[a, q][0][:].rearrange("p t n -> p n t")
+            nc.gpsimd.tensor_tensor(parts[a, q][:, 1, rest], source[:, rest], parts[a, q][:, 0, rest], ALU.subtract)
 
         def mask(a, q, cols=slice(0, NQ)):
             pairs = parts[a, q][:, 0, cols].rearrange("p n t -> p (n t)").bitcast(I32)
@@ -133,22 +154,14 @@ def tile_list_tabts_gelu_kernel(tc, tab_words, tab_scales, w, ts, b, offs, out):
                                     w_raw[a, q][0][:, :, cols].rearrange("p t (n i) -> p n t i", i=RUN),
                                     parts[a, q][:, 0, cols].rearrange("p (n i) t -> p n t i", i=RUN), ALU.subtract)
 
-        def subtract_on_gpsimd(a, q):
-            rest = slice(VECTOR_COLUMNS, NQ)
-            nc.gpsimd.tensor_tensor(parts[a, q][:, 1, rest], w_woven[a, q][:, rest], parts[a, q][:, 0, rest], ALU.subtract)
-
-        def subtract_share(a, q):
-            own = slice(0, VECTOR_COLUMNS)
-            nc.vector.tensor_tensor(parts[a, q][:, 1, own], w_woven[a, q][:, own], parts[a, q][:, 0, own], ALU.subtract)
-
         def quantize(a, q, first=0, last=2):
             cols = slice(first * NQ, last * NQ)
             nc.vector.quantize_mx(out=w_codes[a, q][:, cols].bitcast(FP8X4), scales=w_scales[a, q][:, cols],
                                   in_=parts[a, q][:, first:last].rearrange("p s n t -> p (s n t)"))
 
-        def multiply(a, q, first=0, last=2):
-            for h in range(HALVES):
-                for i in range(NQ // P):
+        def multiply(a, q, first=0, last=2, halves=range(HALVES), groups=range(NQ // P)):
+            for h in halves:
+                for i in groups:
                     if a == 0 and first == 0:
                         sums[q, h, i] = bank(4 * (q % 2) + 2 * h + i, [P, JH], "sum%d%d%d" % (q, h, i))
                     for s in range(first, last):
@@ -160,24 +173,59 @@ def tile_list_tabts_gelu_kernel(tc, tab_words, tab_scales, w, ts, b, offs, out):
                                             start=(a == 0 and s == 0), stop=(a == PASSES - 1 and s == 1))
 
         def scale(q, h, i, cols=slice(0, JH)):
-            nc.vector.tensor_tensor(staged[q][:, 2 * h + i, cols], ts_picked[:, h * JH + cols.start:h * JH + cols.stop], sums[q, h, i][:, cols],
+            nc.vector.tensor_tensor(staged[q, h, i][:, cols], ts_picked[:, h * JH + cols.start:h * JH + cols.stop], sums[q, h, i][:, cols],
                                     ALU.mult)
 
-        def activate(q, h, i, cols=slice(0, JH), queue=nc.sync):
+        def activate(q, h, i, cols=slice(0, JH), queue=nc.sync, source=None):
             r = q * (NQ // P) + i
             result = work.tile([P, cols.stop - cols.start], F32, name="result")
-            nc.scalar.activation(result[:], staged[q][:, 2 * h + i, cols], ACT.Gelu_apprx_tanh, bias=bias[:, r:r + 1])
+            if source is None:
+                source = staged[q, h, i][:, cols]
+            nc.scalar.activation(result[:], source, ACT.Gelu_apprx_tanh, bias=bias[:, r:r + 1])
             queue.dma_start(out=out[r * P:(r + 1) * P, h * JH + cols.start:h * JH + cols.stop], in_=result[:])
 
-        def scale_quarter(q):
-            for h in range(HALVES):
-                for i in range(NQ // P):
-                    scale(q, h, i)
+        def scale_tile(q, h):
+            for i in range(NQ // P):
+                scale(q, h, i)
 
-        def activate_quarter(q):
-            for h in range(HALVES):
-                for i in range(NQ // P):
-                    activate(q, h, i)
+        def activate_tile(q, h):
+            for i in range(NQ // P):
+                activate(q, h, i)
+
+        def gather_ts(h):
+            nc.vector.tensor_copy(ts_picked[:, half(h)], ts_all[:].indirect(picks(h)))
+
+        def turn_ts():
+            blocks = bank(7, [P, JH // P, P], "ts_blocks")
+            for g in range(JH // P):
+                nc.tensor.transpose(blocks[:, g, :], ts_picked[:, g * P:(g + 1) * P], identity[:])
+            nc.vector.tensor_copy(ts_column[:], blocks[:, :, 0])
+
+        def multiply_turned(a, q, first=0, last=2):
+            for g in range(JH // P):
+                if a == 0 and first == 0 and g % 2 == 0:
+                    sums[q, 0, g // 2] = bank(4 * q + g // 2, [P, 2, NQ], "pair%d%d" % (q, g))
+                entries = slice(g * P, (g + 1) * P)
+                for s in range(first, last):
+                    cols = slice(s * NQ, (s + 1) * NQ)
+                    nc.tensor.matmul_mx(out=sums[q, 0, g // 2][:, g % 2, :],
+                                        lhsT=v_codes[a][:, entries].bitcast(FP8X4), lhsT_scale=v_scales[4 * a:, entries],
+                                        rhs=w_codes[a, q][:, cols].bitcast(FP8X4), rhs_scale=w_scales[a, q][:, cols],
+                                        start=(a == 0 and s == 0 and g % 2 == 0),
+                                        stop=(a == PASSES - 1 and s == 1 and g % 2 == 1))
+
+        def scale_turned(q):
+            for g in range(JH // P):
+                nc.scalar.activation(turned[q][:, g, :], sums[q, 0, g // 2][:, g % 2, :], ACT.Copy,
+                                     scale=ts_column[:, g:g + 1])
+
+        def finish_turned(q):
+            back = [bank(4 * q + i, [P, JH], "back%d%d" % (q, i)) for i in range(NQ // P)]
+            for i in range(NQ // P):
+                for g in range(JH // P):
+                    nc.tensor.transpose(back[i][:, g * P:(g + 1) * P], turned[q][:, g, i * P:(i + 1) * P], identity[:])
+            for i in range(NQ // P):
+                activate(q, 0, i, source=back[i][:])
 
         nc.gpsimd.memset(table_scales[:, :T // 8], 0)
         nc.vector.memset(table_scales[:, T // 8:], 0)
@@ -189,82 +237,85 @@ def tile_list_tabts_gelu_kernel(tc, tab_words, tab_scales, w, ts, b, offs, out):
         nc.sync.dma_start(offsets[:], offs)
         load_w(0, 0)
         load_scales()
+        load_bias()
+        turn_bias()
         load_w(1, 0)
         load_words(0)
-        load_bias()
         load_w(0, 1)
         load_words(1)
         load_w(1, 1)
         nc.sync.dma_start(out=ts_all[:], in_=ts)
         for a, q in chunks[4:]:
             load_w(a, q)
-        turn_bias()
-
         truncate(0, 0, nc.vector.tensor_copy)
+        weave(0, 0)
         for a, q in chunks[1:4]:
             truncate(a, q)
-        mask(0, 0, slice(0, VECTOR_COLUMNS))
-        mask(0, 0, slice(VECTOR_COLUMNS, NQ))
-        subtract(0, 0, slice(0, VECTOR_COLUMNS))
-        subtract_on_gpsimd(0, 0)
-        nc.vector.tensor_copy(v_scales[:], table_scales[:].bitcast(U8).indirect(offsets[:]))
-        mask(1, 0)
-        subtract_on_gpsimd(1, 0)
-        quantize(0, 0)
-        subtract_share(1, 0)
-        gather_words(0, 0)
-        gather_words(0, 1)
-        multiply(0, 0)
-        mask(0, 1)
-        subtract_on_gpsimd(0, 1)
-        quantize(1, 0)
-        subtract_share(0, 1)
-        gather_words(1, 0)
-        gather_words(1, 1)
-        multiply(1, 0)
-        mask(1, 1)
-        subtract_on_gpsimd(1, 1)
-        quantize(0, 1)
-        subtract_share(1, 1)
-        nc.vector.tensor_copy(ts_picked[:], ts_all[:].indirect(offsets[:]))
-        multiply(0, 1)
+            weave(a, q)
         truncate(0, 2)
         truncate(1, 2)
-        mask(0, 2)
-        subtract_on_gpsimd(0, 2)
+
+        split(0, 0)
+        nc.vector.tensor_copy(v_scales[:], table_scales[:].bitcast(U8).indirect(offsets[:]))
+        quantize(0, 0)
+        split(1, 0)
+        gather_words(0, 0)
+        multiply_turned(0, 0)
+        gather_words(0, 1)
+        multiply(0, 0, halves=[1])
+        quantize(1, 0)
+        split(0, 1)
+        gather_words(1, 0)
+        multiply_turned(1, 0)
+        gather_words(1, 1)
+        multiply(1, 0, halves=[1])
+        quantize(0, 1)
+        multiply(0, 1, halves=[0])
+        multiply(0, 1, halves=[1], groups=[0])
+        split(1, 1)
+        gather_ts(0)
+        gather_ts(1)
+        turn_ts()
         quantize(1, 1)
-        subtract_share(0, 2)
-        multiply(1, 1)
-        scale_quarter(0)
-        activate_quarter(0)
+        multiply(1, 1, halves=[0])
+        split(0, 2)
+        scale_turned(0)
         truncate(0, 3)
+        finish_turned(0)
+        multiply(0, 1, halves=[1], groups=[1])
+        multiply(1, 1, halves=[1])
         truncate(1, 3)
+        scale_tile(0, 1)
+        scale_tile(1, 0)
+        activate_tile(0, 1)
+        activate_tile(1, 0)
         mask(1, 2)
-        subtract_on_gpsimd(1, 2)
         quantize(0, 2)
-        subtract_share(1, 2)
-        multiply(0, 2)
+        multiply(0, 2, halves=[1, 0])
         quantize(1, 2, 0, 1)
-        multiply(1, 2, 0, 1)
-        scale_quarter(1)
-        activate_quarter(1)
-        mask(0, 3)
+        subtract(1, 2)
+        mask(0, 3, slice(0, PLAIN_SHARE))
+        mask(0, 3, slice(PLAIN_SHARE, NQ))
         quantize(1, 2, 1, 2)
-        multiply(1, 2, 1, 2)
+        multiply(1, 2)
+        subtract(0, 3, slice(0, PLAIN_SHARE))
+        subtract_rest(0, 3)
         quantize(0, 3, 0, 1)
+        scale_tile(1, 1)
+        scale_tile(2, 0)
+        activate_tile(1, 1)
+        activate_tile(2, 0)
         multiply(0, 3, 0, 1)
-        subtract(0, 3)
         mask(1, 3)
-        subtract_on_gpsimd(1, 3)
         quantize(0, 3, 1, 2)
-        subtract_share(1, 3)
         multiply(0, 3, 1, 2)
         quantize(1, 3, 0, 1)
-        multiply(1, 3, 0, 1)
-        scale_quarter(2)
-        activate_quarter(2)
+        subtract(1, 3)
+        scale(2, 1, 0)
         quantize(1, 3, 1, 2)
-        multiply(1, 3, 1, 2)
+        multiply(1, 3)
+        scale(2, 1, 1)
+        activate_tile(2, 1)
         for h, i in ((0, 0), (0, 1), (1, 0)):
             scale(3, h, i)
             activate(3, h, i)

@@ -29,7 +29,7 @@ RESULT_BUFS = 8
 BANK_BYTES = 4 * JH
 KB = 1024
 WOVEN_SHARE = NQ // 8
-PLAIN_SHARE = NQ // 4
+PLAIN_SHARE = NQ // 2
 
 
 def tile_list_tabts_gelu_kernel(tc, tab_words, tab_scales, w, ts, b, offs, out):
@@ -43,9 +43,9 @@ def tile_list_tabts_gelu_kernel(tc, tab_words, tab_scales, w, ts, b, offs, out):
         chunks = [(a, q) for q in range(QUARTERS) for a in range(PASSES)]
         place = {
             "upper02": 0, "staged0": 0,
-            "parts12": 10, "w_raw02": 12,
+            "w_woven02": 44, "parts12": 46, "ts_column": 48, "w_codes02": 50, "parts03": 52,
             "upper03": 16, "staged1": 16,
-            "parts13": 24, "w_raw03": 26,
+            "parts13": 24, "w_woven03": 26, "upper13": 32, "staged2": 32,
         }
 
         def sbuf(name, shape, dtype):
@@ -61,7 +61,7 @@ def tile_list_tabts_gelu_kernel(tc, tab_words, tab_scales, w, ts, b, offs, out):
         bias = sbuf("bias", [P, M // P], F32)
         warm = sbuf("warm", [P, 8], F32)
         identity = sbuf("identity", [P, P], F32)
-        woven_chunks = chunks[:4]
+        woven_chunks = chunks[:5] + [(0, 3)]
         w_raw = {c: [sbuf("w_raw%d%d" % c, [P, PACK, NQ], F32)] for c in chunks}
         upper = {c: sbuf("upper%d%d" % c, [P, 1, NQ, PACK], BF16)[:, 0] for c in chunks}
         parts = {c: sbuf("parts%d%d" % c, [P, 2, NQ, PACK], BF16) for c in chunks}
@@ -70,7 +70,7 @@ def tile_list_tabts_gelu_kernel(tc, tab_words, tab_scales, w, ts, b, offs, out):
         w_scales = {c: sbuf("w_scales%d%d" % c, [P, 2 * NQ], U8) for c in chunks}
         v_codes = [sbuf("v_codes%d" % a, [P, S], U32) for a in range(PASSES)]
         v_scales = sbuf("v_scales", [P, S], U8)
-        ts_picked = sbuf("ts_picked", [P, S], F32)
+        ts_picked = [sbuf("ts_picked%d" % h, [P, JH], F32) for h in range(HALVES)]
         groups = [[(0, 1), (1, 0)], [(1, 1), (2, 0)], [(2, 1), (3, 0)], [(3, 1)]]
         staged = {}
         for n, tiles in enumerate(groups):
@@ -78,7 +78,7 @@ def tile_list_tabts_gelu_kernel(tc, tab_words, tab_scales, w, ts, b, offs, out):
             for m, (q, h) in enumerate(tiles):
                 for i in range(NQ // P):
                     staged[q, h, i] = area[:, 2 * m + i]
-        ts_column = sbuf("ts_column", [P, JH // P], F32)
+        ts_column = sbuf("ts_column", [P, 2 * KB], F32)[:, :JH // P]
         turned = [sbuf("turned%d" % q, [P, JH // P, NQ], F32) for q in range(2)]
 
         def bank(number, shape, name):
@@ -159,6 +159,11 @@ def tile_list_tabts_gelu_kernel(tc, tab_words, tab_scales, w, ts, b, offs, out):
             nc.vector.quantize_mx(out=w_codes[a, q][:, cols].bitcast(FP8X4), scales=w_scales[a, q][:, cols],
                                   in_=parts[a, q][:, first:last].rearrange("p s n t -> p (s n t)"))
 
+        def quantize_lo(a, q, i):
+            cols = slice(NQ + i * P, NQ + (i + 1) * P)
+            nc.vector.quantize_mx(out=w_codes[a, q][:, cols].bitcast(FP8X4), scales=w_scales[a, q][:, cols],
+                                  in_=parts[a, q][:, 1, i * P:(i + 1) * P].rearrange("p n t -> p (n t)"))
+
         def multiply(a, q, first=0, last=2, halves=range(HALVES), groups=range(NQ // P)):
             for h in halves:
                 for i in groups:
@@ -173,7 +178,7 @@ def tile_list_tabts_gelu_kernel(tc, tab_words, tab_scales, w, ts, b, offs, out):
                                             start=(a == 0 and s == 0), stop=(a == PASSES - 1 and s == 1))
 
         def scale(q, h, i, cols=slice(0, JH)):
-            nc.vector.tensor_tensor(staged[q, h, i][:, cols], ts_picked[:, h * JH + cols.start:h * JH + cols.stop], sums[q, h, i][:, cols],
+            nc.vector.tensor_tensor(staged[q, h, i][:, cols], ts_picked[h][:, cols], sums[q, h, i][:, cols],
                                     ALU.mult)
 
         def activate(q, h, i, cols=slice(0, JH), queue=nc.sync, source=None):
@@ -193,13 +198,13 @@ def tile_list_tabts_gelu_kernel(tc, tab_words, tab_scales, w, ts, b, offs, out):
                 activate(q, h, i)
 
         def gather_ts(h):
-            nc.vector.tensor_copy(ts_picked[:, half(h)], ts_all[:].indirect(picks(h)))
+            nc.vector.tensor_copy(ts_picked[h][:], ts_all[:].indirect(picks(h)))
 
         def turn_ts():
             blocks = bank(7, [P, JH // P, P], "ts_blocks")
             for g in range(JH // P):
-                nc.tensor.transpose(blocks[:, g, :], ts_picked[:, g * P:(g + 1) * P], identity[:])
-            nc.vector.tensor_copy(ts_column[:], blocks[:, :, 0])
+                nc.tensor.transpose(blocks[:, g, :], ts_picked[0][:, g * P:(g + 1) * P], identity[:])
+            nc.scalar.copy(out=ts_column, in_=blocks[:, :, 0])
 
         def multiply_turned(a, q, first=0, last=2):
             for g in range(JH // P):
@@ -234,8 +239,8 @@ def tile_list_tabts_gelu_kernel(tc, tab_words, tab_scales, w, ts, b, offs, out):
         nc.gpsimd.memset(bias_rows[:], 0.0)
         make_identity(nc, identity[:])
 
-        nc.sync.dma_start(offsets[:], offs)
         load_w(0, 0)
+        nc.sync.dma_start(offsets[:], offs)
         load_scales()
         load_bias()
         turn_bias()
@@ -253,6 +258,7 @@ def tile_list_tabts_gelu_kernel(tc, tab_words, tab_scales, w, ts, b, offs, out):
             truncate(a, q)
             weave(a, q)
         truncate(0, 2)
+        weave(0, 2)
         truncate(1, 2)
 
         split(0, 0)
@@ -265,25 +271,33 @@ def tile_list_tabts_gelu_kernel(tc, tab_words, tab_scales, w, ts, b, offs, out):
         multiply(0, 0, halves=[1])
         quantize(1, 0)
         split(0, 1)
+        quantize(0, 1, 0, 1)
+        multiply(0, 1, 0, 1, halves=[0])
+        multiply(0, 1, 0, 1, halves=[1], groups=[0])
         gather_words(1, 0)
         multiply_turned(1, 0)
         gather_words(1, 1)
         multiply(1, 0, halves=[1])
-        quantize(0, 1)
-        multiply(0, 1, halves=[0])
-        multiply(0, 1, halves=[1], groups=[0])
+        quantize(0, 1, 1, 2)
+        multiply(0, 1, 1, 2, halves=[0])
+        multiply(0, 1, 1, 2, halves=[1], groups=[0])
         split(1, 1)
+        quantize(1, 1, 0, 1)
+        multiply(1, 1, 0, 1, halves=[0])
+        multiply(1, 1, 0, 1, halves=[1], groups=[0])
         gather_ts(0)
         gather_ts(1)
         turn_ts()
-        quantize(1, 1)
-        multiply(1, 1, halves=[0])
+        multiply(0, 1, halves=[1], groups=[1])
+        multiply(1, 1, 0, 1, halves=[1], groups=[1])
+        quantize(1, 1, 1, 2)
+        multiply(1, 1, 1, 2, halves=[0])
         split(0, 2)
         scale_turned(0)
         truncate(0, 3)
         finish_turned(0)
-        multiply(0, 1, halves=[1], groups=[1])
-        multiply(1, 1, halves=[1])
+        weave(0, 3)
+        multiply(1, 1, 1, 2, halves=[1])
         truncate(1, 3)
         scale_tile(0, 1)
         scale_tile(1, 0)
@@ -294,11 +308,11 @@ def tile_list_tabts_gelu_kernel(tc, tab_words, tab_scales, w, ts, b, offs, out):
         multiply(0, 2, halves=[1, 0])
         quantize(1, 2, 0, 1)
         subtract(1, 2)
-        mask(0, 3, slice(0, PLAIN_SHARE))
-        mask(0, 3, slice(PLAIN_SHARE, NQ))
+        mask(0, 3, slice(0, WOVEN_SHARE))
+        mask(0, 3, slice(WOVEN_SHARE, NQ))
         quantize(1, 2, 1, 2)
         multiply(1, 2)
-        subtract(0, 3, slice(0, PLAIN_SHARE))
+        subtract(0, 3, slice(0, WOVEN_SHARE))
         subtract_rest(0, 3)
         quantize(0, 3, 0, 1)
         scale_tile(1, 1)
@@ -306,19 +320,22 @@ def tile_list_tabts_gelu_kernel(tc, tab_words, tab_scales, w, ts, b, offs, out):
         activate_tile(1, 1)
         activate_tile(2, 0)
         multiply(0, 3, 0, 1)
-        mask(1, 3)
+        mask(1, 3, slice(0, PLAIN_SHARE))
         quantize(0, 3, 1, 2)
         multiply(0, 3, 1, 2)
+        subtract(1, 3, slice(0, PLAIN_SHARE))
+        mask(1, 3, slice(PLAIN_SHARE, NQ))
+        subtract_rest(1, 3)
+        quantize_lo(1, 3, 0)
         quantize(1, 3, 0, 1)
-        subtract(1, 3)
-        scale(2, 1, 0)
-        quantize(1, 3, 1, 2)
-        multiply(1, 3)
-        scale(2, 1, 1)
+        multiply(1, 3, groups=[0])
+        scale_tile(2, 1)
+        scale(3, 0, 0)
         activate_tile(2, 1)
-        for h, i in ((0, 0), (0, 1), (1, 0)):
-            scale(3, h, i)
-            activate(3, h, i)
-        for cols, queue in ((slice(0, JH // 2), nc.sync), (slice(JH // 2, JH), nc.scalar)):
-            scale(3, 1, 1, cols)
-            activate(3, 1, 1, cols, queue)
+        activate(3, 0, 0)
+        quantize_lo(1, 3, 1)
+        multiply(1, 3, groups=[1])
+        for h, i in ((1, 0), (0, 1), (1, 1)):
+            for cols in (slice(0, JH // 2), slice(JH // 2, JH)):
+                scale(3, h, i, cols)
+                activate(3, h, i, cols, nc.scalar if (h, i, cols.stop) == (1, 1, JH) else nc.sync)

@@ -29,7 +29,7 @@ RESULT_BUFS = 8
 BANK_BYTES = 4 * JH
 KB = 1024
 WOVEN_SHARE = NQ // 8
-PLAIN_SHARE = NQ // 2
+PLAIN_SHARE = NQ // 4
 
 
 def tile_list_tabts_gelu_kernel(tc, tab_words, tab_scales, w, ts, b, offs, out):
@@ -43,9 +43,9 @@ def tile_list_tabts_gelu_kernel(tc, tab_words, tab_scales, w, ts, b, offs, out):
         chunks = [(a, q) for q in range(QUARTERS) for a in range(PASSES)]
         place = {
             "upper02": 0, "staged0": 0,
-            "w_woven02": 44, "parts12": 46, "ts_column": 48, "w_codes02": 50, "parts03": 52,
+            "w_raw02": 44, "parts12": 46, "ts_column": 48, "w_codes02": 50, "parts03": 52,
             "upper03": 16, "staged1": 16,
-            "parts13": 24, "w_woven03": 26, "upper13": 32, "staged2": 32,
+            "parts13": 24, "w_raw03": 26, "upper13": 32, "staged2": 32,
         }
 
         def sbuf(name, shape, dtype):
@@ -61,7 +61,7 @@ def tile_list_tabts_gelu_kernel(tc, tab_words, tab_scales, w, ts, b, offs, out):
         bias = sbuf("bias", [P, M // P], F32)
         warm = sbuf("warm", [P, 8], F32)
         identity = sbuf("identity", [P, P], F32)
-        woven_chunks = chunks[:5] + [(0, 3)]
+        woven_chunks = chunks[:4]
         w_raw = {c: [sbuf("w_raw%d%d" % c, [P, PACK, NQ], F32)] for c in chunks}
         upper = {c: sbuf("upper%d%d" % c, [P, 1, NQ, PACK], BF16)[:, 0] for c in chunks}
         parts = {c: sbuf("parts%d%d" % c, [P, 2, NQ, PACK], BF16) for c in chunks}
@@ -121,6 +121,8 @@ def tile_list_tabts_gelu_kernel(tc, tab_words, tab_scales, w, ts, b, offs, out):
             nc.vector.tensor_copy(v_codes[a][:, half(h)], table_words[a][:].bitcast(U32).indirect(picks(h)))
 
         def share(a, q):
+            if (a, q) == chunks[-1]:
+                return P
             return WOVEN_SHARE if (a, q) in w_woven else PLAIN_SHARE
 
         def truncate(a, q, copy=nc.scalar.copy):
@@ -159,10 +161,11 @@ def tile_list_tabts_gelu_kernel(tc, tab_words, tab_scales, w, ts, b, offs, out):
             nc.vector.quantize_mx(out=w_codes[a, q][:, cols].bitcast(FP8X4), scales=w_scales[a, q][:, cols],
                                   in_=parts[a, q][:, first:last].rearrange("p s n t -> p (s n t)"))
 
-        def quantize_lo(a, q, i):
-            cols = slice(NQ + i * P, NQ + (i + 1) * P)
-            nc.vector.quantize_mx(out=w_codes[a, q][:, cols].bitcast(FP8X4), scales=w_scales[a, q][:, cols],
-                                  in_=parts[a, q][:, 1, i * P:(i + 1) * P].rearrange("p n t -> p (n t)"))
+        def quantize_group(a, q, i):
+            for s in range(2):
+                cols = slice(s * NQ + i * P, s * NQ + (i + 1) * P)
+                nc.vector.quantize_mx(out=w_codes[a, q][:, cols].bitcast(FP8X4), scales=w_scales[a, q][:, cols],
+                                      in_=parts[a, q][:, s, i * P:(i + 1) * P].rearrange("p n t -> p (n t)"))
 
         def multiply(a, q, first=0, last=2, halves=range(HALVES), groups=range(NQ // P)):
             for h in halves:
@@ -258,7 +261,6 @@ def tile_list_tabts_gelu_kernel(tc, tab_words, tab_scales, w, ts, b, offs, out):
             truncate(a, q)
             weave(a, q)
         truncate(0, 2)
-        weave(0, 2)
         truncate(1, 2)
 
         split(0, 0)
@@ -271,33 +273,25 @@ def tile_list_tabts_gelu_kernel(tc, tab_words, tab_scales, w, ts, b, offs, out):
         multiply(0, 0, halves=[1])
         quantize(1, 0)
         split(0, 1)
-        quantize(0, 1, 0, 1)
-        multiply(0, 1, 0, 1, halves=[0])
-        multiply(0, 1, 0, 1, halves=[1], groups=[0])
         gather_words(1, 0)
         multiply_turned(1, 0)
         gather_words(1, 1)
         multiply(1, 0, halves=[1])
-        quantize(0, 1, 1, 2)
-        multiply(0, 1, 1, 2, halves=[0])
-        multiply(0, 1, 1, 2, halves=[1], groups=[0])
+        quantize(0, 1)
+        multiply(0, 1, halves=[0])
+        multiply(0, 1, halves=[1], groups=[0])
         split(1, 1)
-        quantize(1, 1, 0, 1)
-        multiply(1, 1, 0, 1, halves=[0])
-        multiply(1, 1, 0, 1, halves=[1], groups=[0])
         gather_ts(0)
         gather_ts(1)
         turn_ts()
         multiply(0, 1, halves=[1], groups=[1])
-        multiply(1, 1, 0, 1, halves=[1], groups=[1])
-        quantize(1, 1, 1, 2)
-        multiply(1, 1, 1, 2, halves=[0])
+        quantize(1, 1)
+        multiply(1, 1, halves=[0])
         split(0, 2)
         scale_turned(0)
         truncate(0, 3)
         finish_turned(0)
-        weave(0, 3)
-        multiply(1, 1, 1, 2, halves=[1])
+        multiply(1, 1, halves=[1])
         truncate(1, 3)
         scale_tile(0, 1)
         scale_tile(1, 0)
@@ -308,11 +302,11 @@ def tile_list_tabts_gelu_kernel(tc, tab_words, tab_scales, w, ts, b, offs, out):
         multiply(0, 2, halves=[1, 0])
         quantize(1, 2, 0, 1)
         subtract(1, 2)
-        mask(0, 3, slice(0, WOVEN_SHARE))
-        mask(0, 3, slice(WOVEN_SHARE, NQ))
+        mask(0, 3, slice(0, PLAIN_SHARE))
+        mask(0, 3, slice(PLAIN_SHARE, NQ))
         quantize(1, 2, 1, 2)
         multiply(1, 2)
-        subtract(0, 3, slice(0, WOVEN_SHARE))
+        subtract(0, 3, slice(0, PLAIN_SHARE))
         subtract_rest(0, 3)
         quantize(0, 3, 0, 1)
         scale_tile(1, 1)
@@ -320,20 +314,19 @@ def tile_list_tabts_gelu_kernel(tc, tab_words, tab_scales, w, ts, b, offs, out):
         activate_tile(1, 1)
         activate_tile(2, 0)
         multiply(0, 3, 0, 1)
-        mask(1, 3, slice(0, PLAIN_SHARE))
+        mask(1, 3, slice(0, P))
         quantize(0, 3, 1, 2)
         multiply(0, 3, 1, 2)
-        subtract(1, 3, slice(0, PLAIN_SHARE))
-        mask(1, 3, slice(PLAIN_SHARE, NQ))
+        subtract(1, 3, slice(0, P))
+        quantize_group(1, 3, 0)
+        mask(1, 3, slice(P, NQ))
         subtract_rest(1, 3)
-        quantize_lo(1, 3, 0)
-        quantize(1, 3, 0, 1)
         multiply(1, 3, groups=[0])
         scale_tile(2, 1)
         scale(3, 0, 0)
         activate_tile(2, 1)
         activate(3, 0, 0)
-        quantize_lo(1, 3, 1)
+        quantize_group(1, 3, 1)
         multiply(1, 3, groups=[1])
         for h, i in ((1, 0), (0, 1), (1, 1)):
             for cols in (slice(0, JH // 2), slice(JH // 2, JH)):

@@ -28,7 +28,7 @@ HI_MASK = 0xFFF0FFF0 - (1 << 32)
 RESULT_BUFS = 8
 BANK_BYTES = 4 * JH
 KB = 1024
-WOVEN_SHARE = NQ // 8
+WOVEN_SHARE = 24
 PLAIN_SHARE = NQ // 4
 
 
@@ -125,9 +125,10 @@ def tile_list_tabts_gelu_kernel(tc, tab_words, tab_scales, w, ts, b, offs, out):
                 return P
             return WOVEN_SHARE if (a, q) in w_woven else PLAIN_SHARE
 
-        def truncate(a, q, copy=nc.scalar.copy):
+        def truncate(a, q, copy=nc.scalar.copy, cols=slice(0, NQ)):
             halves = w_raw[a, q][0][:].bitcast(BF16).rearrange("p t (n i e) -> p n t i e", i=RUN, e=2)[:, :, :, :, 1]
-            copy(out=upper[a, q].rearrange("p (n i) t -> p n t i", i=RUN), in_=halves)
+            copy(out=upper[a, q][:, cols].rearrange("p (n i) t -> p n t i", i=RUN),
+                 in_=halves[:, cols.start // RUN:cols.stop // RUN])
 
         def weave(a, q):
             cols = slice(share(a, q), NQ)
@@ -161,8 +162,8 @@ def tile_list_tabts_gelu_kernel(tc, tab_words, tab_scales, w, ts, b, offs, out):
             nc.vector.quantize_mx(out=w_codes[a, q][:, cols].bitcast(FP8X4), scales=w_scales[a, q][:, cols],
                                   in_=parts[a, q][:, first:last].rearrange("p s n t -> p (s n t)"))
 
-        def quantize_group(a, q, i):
-            for s in range(2):
+        def quantize_group(a, q, i, first=0, last=2):
+            for s in range(first, last):
                 cols = slice(s * NQ + i * P, s * NQ + (i + 1) * P)
                 nc.vector.quantize_mx(out=w_codes[a, q][:, cols].bitcast(FP8X4), scales=w_scales[a, q][:, cols],
                                       in_=parts[a, q][:, s, i * P:(i + 1) * P].rearrange("p n t -> p (n t)"))
@@ -255,7 +256,8 @@ def tile_list_tabts_gelu_kernel(tc, tab_words, tab_scales, w, ts, b, offs, out):
         nc.sync.dma_start(out=ts_all[:], in_=ts)
         for a, q in chunks[4:]:
             load_w(a, q)
-        truncate(0, 0, nc.vector.tensor_copy)
+        truncate(0, 0, cols=slice(0, WOVEN_SHARE))
+        truncate(0, 0, nc.vector.tensor_copy, slice(WOVEN_SHARE, NQ))
         weave(0, 0)
         for a, q in chunks[1:4]:
             truncate(a, q)
@@ -318,9 +320,10 @@ def tile_list_tabts_gelu_kernel(tc, tab_words, tab_scales, w, ts, b, offs, out):
         quantize(0, 3, 1, 2)
         multiply(0, 3, 1, 2)
         subtract(1, 3, slice(0, P))
-        quantize_group(1, 3, 0)
+        quantize_group(1, 3, 0, 0, 1)
         mask(1, 3, slice(P, NQ))
         subtract_rest(1, 3)
+        quantize_group(1, 3, 0, 1, 2)
         multiply(1, 3, groups=[0])
         scale_tile(2, 1)
         scale(3, 0, 0)

@@ -29,7 +29,7 @@ RESULT_BUFS = 8
 BANK_BYTES = 4 * JH
 KB = 1024
 WOVEN_SHARE = 24
-PLAIN_SHARE = NQ // 4
+PLAIN_SHARE = 24
 
 
 def tile_list_tabts_gelu_kernel(tc, tab_words, tab_scales, w, ts, b, offs, out):

@@ -144,18 +144,21 @@ def tile_list_tabts_gelu_kernel(tc, tab_words, tab_scales, w, ts, b, offs, out):
 
         def subtract_rest(a, q):
             rest = slice(share(a, q), NQ)
-            source = w_woven[a, q][:] if (a, q) in w_woven else w_raw[a, q][0][:].rearrange("p t n -> p n t")
-            nc.gpsimd.tensor_tensor(parts[a, q][:, 1, rest], source[:, rest], parts[a, q][:, 0, rest], ALU.subtract)
+            if (a, q) in w_woven:
+                nc.gpsimd.tensor_tensor(parts[a, q][:, 1, rest], w_woven[a, q][:, rest], parts[a, q][:, 0, rest],
+                                        ALU.subtract)
+            else:
+                subtract(a, q, rest, nc.gpsimd)
 
         def mask(a, q, cols=slice(0, NQ)):
             pairs = parts[a, q][:, 0, cols].rearrange("p n t -> p (n t)").bitcast(I32)
             source = upper[a, q][:, cols].rearrange("p n t -> p (n t)").bitcast(I32)
             nc.vector.tensor_scalar(pairs, source, HI_MASK, None, ALU.bitwise_and)
 
-        def subtract(a, q, cols=slice(0, NQ)):
-            nc.vector.tensor_tensor(parts[a, q][:, 1, cols].rearrange("p (n i) t -> p n t i", i=RUN),
-                                    w_raw[a, q][0][:, :, cols].rearrange("p t (n i) -> p n t i", i=RUN),
-                                    parts[a, q][:, 0, cols].rearrange("p (n i) t -> p n t i", i=RUN), ALU.subtract)
+        def subtract(a, q, cols=slice(0, NQ), engine=nc.vector):
+            engine.tensor_tensor(parts[a, q][:, 1, cols].rearrange("p (n i) t -> p n t i", i=RUN),
+                                 w_raw[a, q][0][:, :, cols].rearrange("p t (n i) -> p n t i", i=RUN),
+                                 parts[a, q][:, 0, cols].rearrange("p (n i) t -> p n t i", i=RUN), ALU.subtract)
 
         def quantize(a, q, first=0, last=2):
             cols = slice(first * NQ, last * NQ)

@@ -29,7 +29,7 @@ RESULT_BUFS = 8
 BANK_BYTES = 4 * JH
 KB = 1024
 WOVEN_SHARE = 24
-PLAIN_SHARE = 24
+PLAIN_SHARE = 68
 
 
 def tile_list_tabts_gelu_kernel(tc, tab_words, tab_scales, w, ts, b, offs, out):
@@ -43,7 +43,7 @@ def tile_list_tabts_gelu_kernel(tc, tab_words, tab_scales, w, ts, b, offs, out):
         chunks = [(a, q) for q in range(QUARTERS) for a in range(PASSES)]
         place = {
             "upper02": 0, "staged0": 0,
-            "w_raw02": 44, "parts12": 46, "ts_column": 48, "w_codes02": 50, "parts03": 52,
+            "w_woven02": 44, "parts12": 46, "ts_column": 48, "w_codes02": 50, "parts03": 52,
             "upper03": 16, "staged1": 16,
             "parts13": 24, "w_raw03": 26, "upper13": 32, "staged2": 32,
         }
@@ -61,7 +61,7 @@ def tile_list_tabts_gelu_kernel(tc, tab_words, tab_scales, w, ts, b, offs, out):
         bias = sbuf("bias", [P, M // P], F32)
         warm = sbuf("warm", [P, 8], F32)
         identity = sbuf("identity", [P, P], F32)
-        woven_chunks = chunks[:4]
+        woven_chunks = chunks[:5]
         w_raw = {c: [sbuf("w_raw%d%d" % c, [P, PACK, NQ], F32)] for c in chunks}
         upper = {c: sbuf("upper%d%d" % c, [P, 1, NQ, PACK], BF16)[:, 0] for c in chunks}
         parts = {c: sbuf("parts%d%d" % c, [P, 2, NQ, PACK], BF16) for c in chunks}
@@ -262,10 +262,9 @@ def tile_list_tabts_gelu_kernel(tc, tab_words, tab_scales, w, ts, b, offs, out):
         truncate(0, 0, cols=slice(0, WOVEN_SHARE))
         truncate(0, 0, nc.vector.tensor_copy, slice(WOVEN_SHARE, NQ))
         weave(0, 0)
-        for a, q in chunks[1:4]:
+        for a, q in woven_chunks[1:]:
             truncate(a, q)
             weave(a, q)
-        truncate(0, 2)
         truncate(1, 2)
 
         split(0, 0)
@@ -327,13 +326,15 @@ def tile_list_tabts_gelu_kernel(tc, tab_words, tab_scales, w, ts, b, offs, out):
         mask(1, 3, slice(P, NQ))
         subtract_rest(1, 3)
         quantize_group(1, 3, 0, 1, 2)
+        quantize_group(1, 3, 1, 0, 1)
         multiply(1, 3, groups=[0])
+        multiply(1, 3, 0, 1, groups=[1])
         scale_tile(2, 1)
         scale(3, 0, 0)
         activate_tile(2, 1)
         activate(3, 0, 0)
-        quantize_group(1, 3, 1)
-        multiply(1, 3, groups=[1])
+        quantize_group(1, 3, 1, 1, 2)
+        multiply(1, 3, 1, 2, groups=[1])
         for h, i in ((1, 0), (0, 1), (1, 1)):
             for cols in (slice(0, JH // 2), slice(JH // 2, JH)):
                 scale(3, h, i, cols)

@@ -318,15 +318,13 @@ def tile_list_tabts_gelu_kernel(tc, tab_words, tab_scales, w, ts, b, offs, out):
         activate_tile(1, 1)
         activate_tile(2, 0)
         multiply(0, 3, 0, 1)
-        mask(1, 3, slice(0, P))
+        mask(1, 3)
         quantize(0, 3, 1, 2)
         multiply(0, 3, 1, 2)
         subtract(1, 3, slice(0, P))
-        quantize_group(1, 3, 0, 0, 1)
-        mask(1, 3, slice(P, NQ))
         subtract_rest(1, 3)
+        quantize(1, 3, 0, 1)
         quantize_group(1, 3, 0, 1, 2)
-        quantize_group(1, 3, 1, 0, 1)
         multiply(1, 3, groups=[0])
         multiply(1, 3, 0, 1, groups=[1])
         scale_tile(2, 1)

from contextlib import ExitStack

import concourse.mybir as mybir
from concourse.masks import make_identity

K, M, T, S = 1024, 1024, 2048, 1024
FLOPS = 2 * 2 * K * M * S

F32 = mybir.dt.float32
BF16 = mybir.dt.bfloat16
I32 = mybir.dt.int32
U32 = mybir.dt.uint32
U16 = mybir.dt.uint16
U8 = mybir.dt.uint8
FP8X4 = mybir.dt.float8_e4m3fn_x4
ALU = mybir.AluOpType
ACT = mybir.ActivationFunctionType

P = 128
PACK = 4
PASSES = K // (P * PACK)
NQ = 256
QUARTERS = M // NQ
JH = 512
HALVES = S // JH
RUN = 4
HI_MASK = 0xFFF0FFF0 - (1 << 32)
RESULT_BUFS = 8
BANK_BYTES = 4 * JH
KB = 1024
WOVEN_SHARE = 24
PLAIN_SHARE = 68


def tile_list_tabts_gelu_kernel(tc, tab_words, tab_scales, w, ts, b, offs, out):
    nc = tc.nc
    with ExitStack() as ctx:
        keep = ctx.enter_context(tc.tile_pool(name="keep", bufs=1))
        work = ctx.enter_context(tc.tile_pool(name="work", bufs=RESULT_BUFS))
        psum = ctx.enter_context(tc.psum_pool(name="psum", bufs=1))
        arena = ctx.enter_context(tc.tile_pool(name="arena", bufs=1))

        chunks = [(a, q) for q in range(QUARTERS) for a in range(PASSES)]
        place = {
            "upper02": 0, "staged0": 0,
            "w_woven02": 44, "parts12": 46, "ts_column": 48, "w_codes02": 50, "parts03": 52,
            "upper03": 16, "staged1": 16,
            "parts13": 24, "w_raw03": 26, "upper13": 32, "staged2": 32,
        }

        def sbuf(name, shape, dtype):
            if name in place:
                return arena.tile(shape, dtype, name=name, align_bytes=64, offset=place[name] * KB)
            return keep.tile(shape, dtype, name=name, align_bytes=64)

        offsets = keep.tile([P, S // 16], U16, name="offsets")
        table_words = [sbuf("table_words%d" % a, [P, T], I32) for a in range(PASSES)]
        table_scales = sbuf("table_scales", [P, T // 4], I32)
        ts_all = sbuf("ts_all", [P, T], F32)
        bias_rows = sbuf("bias_rows", [P, P], F32)
        bias = sbuf("bias", [P, M // P], F32)
        warm = sbuf("warm", [P, 8], F32)
        identity = sbuf("identity", [P, P], F32)
        woven_chunks = chunks[:5]
        w_raw = {c: [sbuf("w_raw%d%d" % c, [P, PACK, NQ], F32)] for c in chunks}
        upper = {c: sbuf("upper%d%d" % c, [P, 1, NQ, PACK], BF16)[:, 0] for c in chunks}
        parts = {c: sbuf("parts%d%d" % c, [P, 2, NQ, PACK], BF16) for c in chunks}
        w_woven = {c: sbuf("w_woven%d%d" % c, [P, NQ, PACK], F32) for c in woven_chunks}
        w_codes = {c: sbuf("w_codes%d%d" % c, [P, 2 * NQ], U32) for c in chunks}
        w_scales = {c: sbuf("w_scales%d%d" % c, [P, 2 * NQ], U8) for c in chunks}
        v_codes = [sbuf("v_codes%d" % a, [P, S], U32) for a in range(PASSES)]
        v_scales = sbuf("v_scales", [P, S], U8)
        ts_picked = [sbuf("ts_picked%d" % h, [P, JH], F32) for h in range(HALVES)]
        groups = [[(0, 1), (1, 0)], [(1, 1), (2, 0)], [(2, 1), (3, 0)], [(3, 1)]]
        staged = {}
        for n, tiles in enumerate(groups):
            area = sbuf("staged%d" % n, [P, 2 * len(tiles), JH], F32)
            for m, (q, h) in enumerate(tiles):
                for i in range(NQ // P):
                    staged[q, h, i] = area[:, 2 * m + i]
        ts_column = sbuf("ts_column", [P, 2 * KB], F32)[:, :JH // P]
        turned = [sbuf("turned%d" % q, [P, JH // P, NQ], F32) for q in range(2)]

        def bank(number, shape, name):
            return psum.tile(shape, F32, name=name, offset=number * BANK_BYTES)

        sums = {}

        def pieces(a, q):
            width = NQ // len(w_raw[a, q])
            return [(raw, slice(n * width, (n + 1) * width)) for n, raw in enumerate(w_raw[a, q])]

        def load_w(a, q):
            rows = w[a * P * PACK:(a + 1) * P * PACK, q * NQ:(q + 1) * NQ].rearrange("(p t) n -> p t n", t=PACK)
            for raw, cols in pieces(a, q):
                nc.sync.dma_start(out=raw[:], in_=rows[:, :, cols])

        def load_words(a):
            nc.sync.dma_start(out=table_words[a][:], in_=tab_words[a].rearrange("p t i -> p (t i)").bitcast(I32))

        def load_scales():
            for quad in range(4):
                nc.sync.dma_start(out=table_scales[32 * quad:32 * quad + 4 * PASSES, :],
                                  in_=tab_scales[:, 4 * quad:4 * quad + 4, :].bitcast(I32))

        def load_bias():
            nc.sync.dma_start(out=bias_rows[:M // P, :], in_=b.rearrange("(r p) -> r p", p=P))

        def turn_bias():
            turned_bias = bank(3, [P, P], "turned_bias")
            nc.tensor.transpose(turned_bias[:], bias_rows[:], identity[:])
            nc.scalar.copy(out=bias[:], in_=turned_bias[:, :M // P])

        def half(h):
            return slice(h * JH, (h + 1) * JH)

        def picks(h):
            return offsets[:, h * JH // 16:(h + 1) * JH // 16]

        def gather_words(a, h):
            nc.vector.tensor_copy(v_codes[a][:, half(h)], table_words[a][:].bitcast(U32).indirect(picks(h)))

        def share(a, q):
            if (a, q) == chunks[-1]:
                return P
            return WOVEN_SHARE if (a, q) in w_woven else PLAIN_SHARE

        def truncate(a, q, copy=nc.scalar.copy, cols=slice(0, NQ)):
            halves = w_raw[a, q][0][:].bitcast(BF16).rearrange("p t (n i e) -> p n t i e", i=RUN, e=2)[:, :, :, :, 1]
            copy(out=upper[a, q][:, cols].rearrange("p (n i) t -> p n t i", i=RUN),
                 in_=halves[:, cols.start // RUN:cols.stop // RUN])

        def weave(a, q):
            cols = slice(share(a, q), NQ)
            nc.scalar.copy(out=w_woven[a, q][:, cols].rearrange("p (n i) t -> p n t i", i=RUN),
                           in_=w_raw[a, q][0][:, :, cols].rearrange("p t (n i) -> p n t i", i=RUN))

        def split(a, q):
            own, rest = slice(0, share(a, q)), slice(share(a, q), NQ)
            mask(a, q, own)
            mask(a, q, rest)
            subtract(a, q, own)
            subtract_rest(a, q)

        def subtract_rest(a, q):
            rest = slice(share(a, q), NQ)
            if (a, q) in w_woven:
                nc.gpsimd.tensor_tensor(parts[a, q][:, 1, rest], w_woven[a, q][:, rest], parts[a, q][:, 0, rest],
                                        ALU.subtract)
            else:
                subtract(a, q, rest, nc.gpsimd)

        def mask(a, q, cols=slice(0, NQ)):
            pairs = parts[a, q][:, 0, cols].rearrange("p n t -> p (n t)").bitcast(I32)
            source = upper[a, q][:, cols].rearrange("p n t -> p (n t)").bitcast(I32)
            nc.vector.tensor_scalar(pairs, source, HI_MASK, None, ALU.bitwise_and)

        def subtract(a, q, cols=slice(0, NQ), engine=nc.vector):
            engine.tensor_tensor(parts[a, q][:, 1, cols].rearrange("p (n i) t -> p n t i", i=RUN),
                                 w_raw[a, q][0][:, :, cols].rearrange("p t (n i) -> p n t i", i=RUN),
                                 parts[a, q][:, 0, cols].rearrange("p (n i) t -> p n t i", i=RUN), ALU.subtract)

        def quantize(a, q, first=0, last=2):
            cols = slice(first * NQ, last * NQ)
            nc.vector.quantize_mx(out=w_codes[a, q][:, cols].bitcast(FP8X4), scales=w_scales[a, q][:, cols],
                                  in_=parts[a, q][:, first:last].rearrange("p s n t -> p (s n t)"))

        def quantize_group(a, q, i, first=0, last=2):
            for s in range(first, last):
                cols = slice(s * NQ + i * P, s * NQ + (i + 1) * P)
                nc.vector.quantize_mx(out=w_codes[a, q][:, cols].bitcast(FP8X4), scales=w_scales[a, q][:, cols],
                                      in_=parts[a, q][:, s, i * P:(i + 1) * P].rearrange("p n t -> p (n t)"))

        def multiply(a, q, first=0, last=2, halves=range(HALVES), groups=range(NQ // P)):
            for h in halves:
                for i in groups:
                    if a == 0 and first == 0:
                        sums[q, h, i] = bank(4 * (q % 2) + 2 * h + i, [P, JH], "sum%d%d%d" % (q, h, i))
                    for s in range(first, last):
                        cols = slice(s * NQ + i * P, s * NQ + (i + 1) * P)
                        nc.tensor.matmul_mx(out=sums[q, h, i][:], lhsT=w_codes[a, q][:, cols].bitcast(FP8X4),
                                            lhsT_scale=w_scales[a, q][:, cols],
                                            rhs=v_codes[a][:, half(h)].bitcast(FP8X4),
                                            rhs_scale=v_scales[4 * a:, half(h)],
                                            start=(a == 0 and s == 0), stop=(a == PASSES - 1 and s == 1))

        def scale(q, h, i, cols=slice(0, JH)):
            nc.vector.tensor_tensor(staged[q, h, i][:, cols], ts_picked[h][:, cols], sums[q, h, i][:, cols],
                                    ALU.mult)

        def activate(q, h, i, cols=slice(0, JH), queue=nc.sync, source=None):
            r = q * (NQ // P) + i
            result = work.tile([P, cols.stop - cols.start], F32, name="result")
            if source is None:
                source = staged[q, h, i][:, cols]
            nc.scalar.activation(result[:], source, ACT.Gelu_apprx_tanh, bias=bias[:, r:r + 1])
            queue.dma_start(out=out[r * P:(r + 1) * P, h * JH + cols.start:h * JH + cols.stop], in_=result[:])

        def scale_tile(q, h):
            for i in range(NQ // P):
                scale(q, h, i)

        def activate_tile(q, h):
            for i in range(NQ // P):
                activate(q, h, i)

        def gather_ts(h):
            nc.vector.tensor_copy(ts_picked[h][:], ts_all[:].indirect(picks(h)))

        def turn_ts():
            blocks = bank(7, [P, JH // P, P], "ts_blocks")
            for g in range(JH // P):
                nc.tensor.transpose(blocks[:, g, :], ts_picked[0][:, g * P:(g + 1) * P], identity[:])
            nc.scalar.copy(out=ts_column, in_=blocks[:, :, 0])

        def multiply_turned(a, q, first=0, last=2):
            for g in range(JH // P):
                if a == 0 and first == 0 and g % 2 == 0:
                    sums[q, 0, g // 2] = bank(4 * q + g // 2, [P, 2, NQ], "pair%d%d" % (q, g))
                entries = slice(g * P, (g + 1) * P)
                for s in range(first, last):
                    cols = slice(s * NQ, (s + 1) * NQ)
                    nc.tensor.matmul_mx(out=sums[q, 0, g // 2][:, g % 2, :],
                                        lhsT=v_codes[a][:, entries].bitcast(FP8X4), lhsT_scale=v_scales[4 * a:, entries],
                                        rhs=w_codes[a, q][:, cols].bitcast(FP8X4), rhs_scale=w_scales[a, q][:, cols],
                                        start=(a == 0 and s == 0 and g % 2 == 0),
                                        stop=(a == PASSES - 1 and s == 1 and g % 2 == 1))

        def scale_turned(q):
            for g in range(JH // P):
                nc.scalar.activation(turned[q][:, g, :], sums[q, 0, g // 2][:, g % 2, :], ACT.Copy,
                                     scale=ts_column[:, g:g + 1])

        def finish_turned(q):
            back = [bank(4 * q + i, [P, JH], "back%d%d" % (q, i)) for i in range(NQ // P)]
            for i in range(NQ // P):
                for g in range(JH // P):
                    nc.tensor.transpose(back[i][:, g * P:(g + 1) * P], turned[q][:, g, i * P:(i + 1) * P], identity[:])
            for i in range(NQ // P):
                activate(q, 0, i, source=back[i][:])

        nc.gpsimd.memset(table_scales[:, :T // 8], 0)
        nc.vector.memset(table_scales[:, T // 8:], 0)
        nc.gpsimd.memset(warm[:], 0.0)
        nc.scalar.activation(warm[:, 4:5], warm[:, 0:1], ACT.Gelu_apprx_tanh)
        nc.gpsimd.memset(bias_rows[:], 0.0)
        make_identity(nc, identity[:])

        load_w(0, 0)
        nc.sync.dma_start(offsets[:], offs)
        load_scales()
        load_bias()
        turn_bias()
        load_w(1, 0)
        load_words(0)
        load_w(0, 1)
        load_words(1)
        load_w(1, 1)
        nc.sync.dma_start(out=ts_all[:], in_=ts)
        for a, q in chunks[4:]:
            load_w(a, q)
        truncate(0, 0, cols=slice(0, WOVEN_SHARE))
        truncate(0, 0, nc.vector.tensor_copy, slice(WOVEN_SHARE, NQ))
        weave(0, 0)
        for a, q in woven_chunks[1:]:
            truncate(a, q)
            weave(a, q)
        truncate(1, 2)

        split(0, 0)
        nc.vector.tensor_copy(v_scales[:], table_scales[:].bitcast(U8).indirect(offsets[:]))
        quantize(0, 0)
        split(1, 0)
        gather_words(0, 0)
        multiply_turned(0, 0)
        gather_words(0, 1)
        multiply(0, 0, halves=[1])
        quantize(1, 0)
        split(0, 1)
        gather_words(1, 0)
        multiply_turned(1, 0)
        gather_words(1, 1)
        multiply(1, 0, halves=[1])
        quantize(0, 1)
        multiply(0, 1, halves=[0])
        multiply(0, 1, halves=[1], groups=[0])
        split(1, 1)
        gather_ts(0)
        gather_ts(1)
        turn_ts()
        multiply(0, 1, halves=[1], groups=[1])
        quantize(1, 1)
        multiply(1, 1, halves=[0])
        split(0, 2)
        scale_turned(0)
        truncate(0, 3)
        finish_turned(0)
        multiply(1, 1, halves=[1])
        truncate(1, 3)
        scale_tile(0, 1)
        scale_tile(1, 0)
        activate_tile(0, 1)
        activate_tile(1, 0)
        mask(1, 2)
        quantize(0, 2)
        multiply(0, 2, halves=[1, 0])
        quantize(1, 2, 0, 1)
        subtract(1, 2)
        mask(0, 3, slice(0, PLAIN_SHARE))
        mask(0, 3, slice(PLAIN_SHARE, NQ))
        quantize(1, 2, 1, 2)
        multiply(1, 2)
        subtract(0, 3, slice(0, PLAIN_SHARE))
        subtract_rest(0, 3)
        quantize(0, 3, 0, 1)
        scale_tile(1, 1)
        scale_tile(2, 0)
        activate_tile(1, 1)
        activate_tile(2, 0)
        multiply(0, 3, 0, 1)
        mask(1, 3)
        quantize(0, 3, 1, 2)
        multiply(0, 3, 1, 2)
        subtract(1, 3, slice(0, P))
        subtract_rest(1, 3)
        quantize(1, 3, 0, 1)
        quantize_group(1, 3, 0, 1, 2)
        multiply(1, 3, groups=[0])
        multiply(1, 3, 0, 1, groups=[1])
        scale_tile(2, 1)
        scale(3, 0, 0)
        activate_tile(2, 1)
        activate(3, 0, 0)
        quantize_group(1, 3, 1, 1, 2)
        multiply(1, 3, 1, 2, groups=[1])
        for h, i in ((1, 0), (0, 1), (1, 1)):
            for cols in (slice(0, JH // 2), slice(JH // 2, JH)):
                scale(3, h, i, cols)
                activate(3, h, i, cols, nc.scalar if (h, i, cols.stop) == (1, 1, JH) else nc.sync)
